import numpy as np
import ml_dtypes


def mxq(x, axis, fmt="e4m3"):
    dtype, down = {"e4m3": (ml_dtypes.float8_e4m3fn, 7), "e5m2": (ml_dtypes.float8_e5m2, 14)}[fmt]
    v = np.moveaxis(np.asarray(x, np.float32).astype(ml_dtypes.bfloat16).astype(np.float64), axis, -1)
    blocks = v.reshape(v.shape[:-1] + (-1, 32))
    amax = np.abs(blocks).max(-1, keepdims=True)
    byte = np.maximum(np.where(amax > 0, np.frexp(amax)[1] - 1 + 127, 0) - down, 1)
    scale = np.exp2(byte - 127.0)
    codes = (blocks / scale).astype(np.float32).astype(dtype).astype(np.float64)
    return np.moveaxis((codes * scale).reshape(v.shape), -1, axis)


WIDE = False


def mx_kscale(k):
    if not WIDE:
        return np.ones(k)
    levels = np.array([10, -10, 5, -5, 0])
    if k % 512:
        return np.exp2(np.random.permutation(np.resize(levels, k // 32))).repeat(32)
    a = np.empty((k // 512, 16))
    for p in range(k // 512):
        a[p, :8] = np.random.permutation(np.resize(levels, 8))
        for g in range(8):
            far = levels[np.abs(levels - a[p, g]) >= 10]
            a[p, g + 8] = far[np.random.randint(len(far))]
    return np.exp2(a.ravel()).repeat(32)


def f64(x):
    return np.asarray(x).astype(np.float64)


def striped(idx):
    return np.tile(idx.reshape(-1, 16).T, (8, 1)).astype(np.uint16)


def unstriped(offs):
    return offs[:16].T.reshape(-1).astype(np.int64)


E2M1 = np.array([0.0, 0.5, 1.0, 1.5, 2.0, 3.0, 4.0, 6.0, -0.0, -0.5, -1.0, -1.5, -2.0, -3.0, -4.0, -6.0])


def pack_weight(w, fmt):
    k, n = w.shape
    w = f64(np.asarray(w, np.float32).astype(ml_dtypes.bfloat16)).reshape(k // 32, 32, n)
    amax = np.abs(w).max(1)
    if fmt == "e4m3":
        byte = np.frexp(amax)[1] - 1 + 127 - 7
    else:
        mant, ex = np.frexp(amax / 6.0)
        byte = np.where(mant > 0.5, ex, ex - 1) + 127
    byte = np.clip(np.where(amax > 0, byte, 1), 1, 254)
    scaled = (w * np.exp2(127.0 - byte)[:, None, :]).reshape(k, n).astype(np.float32)
    by_word = np.ascontiguousarray(scaled.reshape(k // 512, 128, 4, n).transpose(0, 1, 3, 2))
    if fmt == "e4m3":
        words = by_word.astype(ml_dtypes.float8_e4m3fn).view(np.uint8)
    else:
        c = by_word.astype(ml_dtypes.float4_e2m1fn).view(np.uint8) & 0xF
        words = (c[..., 0::2] | (c[..., 1::2] << 4)).reshape(k // 512, 128, 2 * n)
    return np.ascontiguousarray(words), np.ascontiguousarray(byte.astype(np.uint8).reshape(k // 512, 16, n))


def unpack_weight(words, scales, fmt):
    g, _, n = scales.shape
    words = np.ascontiguousarray(words).reshape(g, 128, n, -1)
    if fmt == "e4m3":
        vals = words.view(ml_dtypes.float8_e4m3fn).astype(np.float64)
    else:
        nib = np.empty((g, 128, n, 4), np.uint8)
        nib[..., 0::2] = words & 0xF
        nib[..., 1::2] = words >> 4
        vals = E2M1[nib]
    vals = vals * np.repeat(np.exp2(scales.astype(np.float64) - 127.0), 8, axis=1)[..., None]
    return vals.transpose(0, 1, 3, 2).reshape(g * 512, n)


def gelu(v):
    return 0.5 * v * (1.0 + np.tanh(np.sqrt(2.0 / np.pi) * (v + 0.044715 * v**3)))


K, T, S, H, T2, P, N = 1024, 2048, 1024, 1024, 2048, 512, 512

def setup_inputs():
    n = np.random.standard_normal
    s = mx_kscale(K)[:, None]
    u = mx_kscale(H)[:, None]
    tab_words, tab_scales = pack_weight(n((K, T)) * s, "e4m3")
    w2_words, w2_scales = pack_weight(n((H, N)) / np.sqrt(H) / u, "e2m1")
    sign = np.where(n(H) > 0, 1.0, -1.0)
    return {
        "tab_words": tab_words, "tab_scales": tab_scales,
        "offs": striped(np.random.permutation(T)[:S]),
        "w1": (0.75 * n((K, H)) / np.sqrt(K) / s).astype(np.float32),
        "low": (0.75 * n((H, S))).astype(np.float32),
        "page0": (0.8 * n((H, T2))).astype(np.float32),
        "wgs": np.exp(0.3 * n((128, S))).astype(np.float32),
        "offs2": striped(np.random.permutation(T2)[:S]),
        "offs3": striped(np.random.permutation(T2)[:P]),
        "cal_s": np.random.uniform(0.6, 3.0, H).astype(np.float32),
        "cal_b": n(H).astype(np.float32),
        "gain1": (sign * np.random.uniform(0.8, 2.5, H) * u[:, 0]).astype(np.float32),
        "ease": (0.5 * n((H, P))).astype(np.float32),
        "gain2": (np.random.uniform(0.8, 2.0, H) * u[:, 0]).astype(np.float32),
        "w2_words": w2_words, "w2_scales": w2_scales,
        "w3": (n((H, N)) / np.sqrt(H) / u).astype(np.float32),
    }

def reference(tab_words, tab_scales, offs, w1, low, page0, wgs, offs2, offs3,
              cal_s, cal_b, gain1, ease, gain2, w2_words, w2_scales, w3):
    v = unpack_weight(tab_words, tab_scales, "e4m3")[:, unstriped(offs)]
    h = np.maximum(mxq(f64(w1), 0, "e4m3").T @ v, f64(low))
    page = f64(page0).copy()
    page[:, unstriped(offs2)] = np.tile(f64(wgs), (H // 128, 1)) * h
    x = 1.0 / (1.0 + np.exp(-(f64(cal_s)[:, None] * page[:, unstriped(offs3)] + f64(cal_b)[:, None])))
    x1 = mxq(f64(gain1)[:, None] * x, 0, "e4m3")
    x2 = mxq(f64(gain2)[:, None] * (x - f64(ease)), 0, "e4m3")
    w2 = unpack_weight(w2_words, w2_scales, "e2m1")
    y1 = w2.T @ x1
    y2 = mxq(f64(w3), 0, "e4m3").T @ x2
    return y1 * y2

@@ -1,0 +1,311 @@
+from contextlib import ExitStack
+
+import concourse.mybir as mybir
+
+K, T, S, H, T2, M, N = 1024, 2048, 1024, 1024, 2048, 512, 512
+FLOPS = 2 * K * H * S + 2 * 2 * H * N * M
+
+F32 = mybir.dt.float32
+BF16 = mybir.dt.bfloat16
+I32 = mybir.dt.int32
+U32 = mybir.dt.uint32
+U16 = mybir.dt.uint16
+U8 = mybir.dt.uint8
+FP8X4 = mybir.dt.float8_e4m3fn_x4
+FP4X4 = mybir.dt.float4_e2m1fn_x4
+ACT = mybir.ActivationFunctionType
+ALU = mybir.AluOpType
+
+P = 128
+PACK = 4
+KP = P * PACK
+BANK = 512
+HALF = M // 2
+H_BYTES = 4 * S
+
+
+def tile_list_tablature_fingering_kernel(tc, tab_words, tab_scales, offs, w1, low, page0, wgs, offs2, offs3,
+                                                   cal_s, cal_b, gain1, ease, gain2, w2_words, w2_scales, w3, out):
+    nc = tc.nc
+    with ExitStack() as ctx:
+        keep = ctx.enter_context(tc.tile_pool(name="keep", bufs=1))
+        ring = ctx.enter_context(tc.tile_pool(name="ring", bufs=4))
+        bfp = ctx.enter_context(tc.tile_pool(name="bfp", bufs=2))
+        hreg = ctx.enter_context(tc.tile_pool(name="hreg", bufs=1))
+        psum = ctx.enter_context(tc.psum_pool(name="psum", bufs=1))
+
+        def rows(mat, i):
+            b, t = divmod(i, PACK)
+            return mat.rearrange("(b p t) c -> b t p c", b=2, t=PACK)[b, t]
+
+        tsc = keep.tile([P, T], U8, name="tsc", align_bytes=64)
+        nc.vector.memset(tsc[:].bitcast(U32), 0)
+        for q in range(4):
+            nc.scalar.dma_start(out=tsc[32 * q : 32 * q + 8, :].bitcast(I32), in_=tab_scales[:, 4 * q : 4 * q + 4, :].bitcast(I32))
+        w2s = keep.tile([P, 2, N], U8, name="w2s", align_bytes=64)
+        nc.gpsimd.memset(w2s[:].rearrange("p a c -> p (a c)").bitcast(U32), 0)
+        for q in range(4):
+            nc.gpsimd.dma_start(out=w2s[32 * q : 32 * q + 4, :, :].bitcast(I32),
+                                in_=w2_scales[:, 4 * q : 4 * q + 4, :].rearrange("a r c -> r a c").bitcast(I32))
+        vec = {}
+        for name, v in (("cal_s", cal_s), ("cal_b", cal_b), ("gain1", gain1), ("gain2", gain2)):
+            vec[name] = keep.tile([P, 2, PACK], F32, name=name)
+            nc.gpsimd.dma_start(out=vec[name][:], in_=v.rearrange("(b p t) -> p b t", b=2, t=PACK))
+
+        def col(name, i):
+            b, t = divmod(i, PACK)
+            return vec[name][:, b, t : t + 1]
+
+        wgs_q = wgs.rearrange("(q t) j -> q t j", t=PACK)
+        wg0 = keep.tile([P, S], F32, name="wg0")
+        for q in (0, 2, 1, 3):
+            nc.scalar.dma_start(out=wg0[32 * q : 32 * q + 32, :], in_=wgs_q[:, 0, :])
+
+        def load_list(src, name):
+            t = keep.tile([P, src.shape[1]], U16, name=name)
+            nc.sync.dma_start(t[:], src)
+            return t
+
+        def load_tab(a):
+            t = keep.tile([P, T], I32, name=f"tabw{a}", tag=f"tab{a}")
+            nc.sync.dma_start(out=t[:], in_=tab_words[a].rearrange("p t i -> p (t i)").bitcast(I32))
+            return t
+
+        def load_raw(src, tag, name):
+            t = keep.tile([P, PACK, 512], F32, name=name, tag=tag)
+            nc.sync.dma_start(out=t[:], in_=src.rearrange("(p j) c -> p j c", j=PACK))
+            return t
+
+        def w1_part(a, b):
+            return w1[KP * a : KP * (a + 1), KP * b : KP * (b + 1)]
+
+        lows, pages, eases, hs, xs = {}, {}, {}, {}, {}
+
+        def load_low(i):
+            if i == 0:
+                lows[i] = keep.tile([P, S], F32, name="low0", tag="low0")
+            else:
+                lows[i] = ring.tile([P, S], F32, name=f"low{i}", tag="low")
+            nc.sync.dma_start(out=lows[i][:], in_=rows(low, i))
+
+        def load_page(i):
+            pages[i] = ring.tile([P, T2], F32, name=f"page{i}", tag="page")
+            nc.sync.dma_start(out=pages[i][:], in_=rows(page0, i))
+
+        def load_ease(i):
+            eases[i] = keep.tile([P, M], F32, name=f"ease{i}")
+            nc.sync.dma_start(out=eases[i][:], in_=rows(ease, i))
+
+        def group_w1(raw, name):
+            g = bfp.tile([P, 2048], BF16, name=name, tag="wbf", align_bytes=64)
+            nc.scalar.copy(out=g[:].rearrange("p (t m j) -> p m j t", t=PACK, j=PACK),
+                           in_=raw[:].rearrange("p j (m t) -> p m j t", t=PACK))
+            return g
+
+        def group_w3(raw, name):
+            g = bfp.tile([P, 2048], BF16, name=name, tag="wbf", align_bytes=64)
+            nc.scalar.copy(out=g[:].rearrange("p (c i j) -> p c j i", i=4, j=PACK),
+                           in_=raw[:].rearrange("p j (c i) -> p c j i", i=4))
+            return g
+
+        def quantise(grouped, name, offset=None):
+            width = grouped.shape[1] // PACK
+            codes = keep.tile([P, width], U32, name=name + "_codes", align_bytes=64)
+            if offset is None:
+                scales = keep.tile([P, width], U8, name=name + "_scales", align_bytes=64)
+            else:
+                scales = hreg.tile([P, width], U8, name=name + "_scales", align_bytes=64, offset=offset)
+            nc.vector.quantize_mx(out=codes[:].bitcast(FP8X4), scales=scales[:], in_=grouped)
+            return codes, scales
+
+        o1 = load_list(offs, "o1")
+        tab0 = load_tab(0)
+        raw00 = load_raw(w1_part(0, 0), "raw0", "raw00")
+        raw10 = load_raw(w1_part(1, 0), "raw1", "raw10")
+        tab1 = load_tab(1)
+        o2 = load_list(offs2, "o2")
+        load_low(0)
+        load_page(0)
+
+        gw = {}
+
+        def gather_words(tab, a, hj):
+            gw[a, hj] = keep.tile([P, BANK], U32, name=f"gw{a}{hj}", align_bytes=64)
+            nc.vector.tensor_copy(out=gw[a, hj][:], in_=tab[:].bitcast(U32).indirect(o1[:, 32 * hj : 32 * hj + 32]))
+
+        gather_words(tab0, 0, 0)
+        gather_words(tab0, 0, 1)
+        gs = keep.tile([P, S], U8, name="gs", align_bytes=64)
+        nc.vector.tensor_copy(out=gs[:], in_=tsc[:].indirect(o1[:]))
+        w1q = {}
+        g00 = group_w1(raw00, "g00")
+        g10 = group_w1(raw10, "g10")
+        w1q[0, 0] = quantise(g00[:], "w1q00")
+        gather_words(tab1, 1, 0)
+        w1q[1, 0] = quantise(g10[:], "w1q10")
+        gather_words(tab1, 1, 1)
+
+        def floor_h(i):
+            b, t = divmod(i, PACK)
+            hs[i] = hreg.tile([P, S], F32, name=f"h{i}", align_bytes=64, offset=H_BYTES * i)
+            for hj in range(2):
+                cols = slice(BANK * hj, BANK * (hj + 1))
+                acc = psum.tile([P, BANK], F32, name=f"hacc{i}_{hj}", tag=f"bank{2 * (i % 4) + hj}")
+                for a in range(2):
+                    codes, scales = w1q[a, b]
+                    nc.tensor.matmul_mx(out=acc[:], lhsT=codes[:, P * t : P * (t + 1)].bitcast(FP8X4), lhsT_scale=scales[:, P * t : P * (t + 1)],
+                                        rhs=gw[a, hj][:].bitcast(FP8X4), rhs_scale=gs[4 * a : P, cols], start=(a == 0), stop=(a == 1))
+                nc.vector.tensor_tensor(out=hs[i][:, cols], in0=acc[:], in1=lows[i][:, cols], op=ALU.max)
+
+        wg = {0: wg0[:]}
+
+        def scatter(i):
+            nc.vector.tensor_tensor(out=pages[i][:].indirect(o2[:]), in0=hs[i][:], in1=wg[i % PACK], op=ALU.mult)
+
+        xi = {}
+        for which in (1, 2):
+            xi[which, 0] = [keep.tile([P, M, PACK], BF16, name=f"xi{which}0", align_bytes=64)]
+            xi[which, 1] = [keep.tile([P, HALF, PACK], BF16, name=f"xi{which}1{hm}", align_bytes=64) for hm in range(2)]
+
+        def plane(which, i, src):
+            b, t = divmod(i, PACK)
+            parts = xi[which, b]
+            w = M // len(parts)
+            for n, part in enumerate(parts):
+                nc.scalar.activation(out=part[:, :, t], in_=src[:, w * n : w * (n + 1)], func=ACT.Copy, scale=col(f"gain{which}", i))
+
+        def look(i):
+            xs[i] = ring.tile([P, M], F32, name=f"x{i}", tag="x")
+            nc.scalar.activation(out=xs[i][:], in_=pages[i][:].indirect(o3[:]), func=ACT.Sigmoid, bias=col("cal_b", i), scale=col("cal_s", i))
+            plane(1, i, xs[i])
+
+        def less_ease(i, offset):
+            d = hreg.tile([P, M], F32, name=f"d{i}", align_bytes=64, offset=offset)
+            nc.vector.tensor_tensor(out=d[:], in0=xs[i][:], in1=eases[i][:], op=ALU.subtract)
+            plane(2, i, d)
+
+        floor_h(0)
+        scatter(0)
+        wg123 = keep.tile([P, 3, S], F32, name="wg123", tag="low0")
+        for q in (0, 2, 1, 3):
+            nc.scalar.dma_start(out=wg123[32 * q : 32 * q + 32, :, :], in_=wgs_q[:, 1:PACK, :])
+        for t in range(1, PACK):
+            wg[t] = wg123[:, t - 1, :]
+
+        load_low(1)
+        load_low(2)
+        load_page(1)
+        floor_h(1)
+        floor_h(2)
+        scatter(1)
+
+        raw01 = load_raw(w1_part(0, 1), "raw1", "raw01")
+        raw11 = load_raw(w1_part(1, 1), "raw0", "raw11")
+        o3 = load_list(offs3, "o3")
+        load_low(3)
+        load_page(2)
+        g01 = group_w1(raw01, "g01")
+        g11 = group_w1(raw11, "g11")
+        look(0)
+        look(1)
+        floor_h(3)
+        scatter(2)
+
+        load_ease(0)
+        load_ease(1)
+        load_page(3)
+        w1q[0, 1] = quantise(g01[:], "w1q01", H_BYTES * 2 + 2048)
+        w1q[1, 1] = quantise(g11[:], "w1q11", H_BYTES * 2 + 2560)
+        look(2)
+        less_ease(0, H_BYTES * 1)
+        less_ease(1, H_BYTES * 2)
+        scatter(3)
+
+        load_ease(2)
+        load_low(4)
+        load_low(5)
+        load_page(4)
+        look(3)
+        less_ease(2, H_BYTES * 3)
+        floor_h(4)
+        floor_h(5)
+        scatter(4)
+
+        load_ease(3)
+        load_low(6)
+        raw30 = load_raw(w3[0:KP, :], "tab0", "raw30")
+        w2w = keep.tile([P, 2, 2 * N], U8, name="w2w", align_bytes=64)
+        nc.sync.dma_start(out=w2w[:].bitcast(I32), in_=w2_words.rearrange("a p c -> p a c").bitcast(I32))
+        load_page(5)
+        look(4)
+        less_ease(3, H_BYTES * 4)
+        floor_h(6)
+        g30 = group_w3(raw30, "g30")
+        scatter(5)
+
+        load_ease(4)
+        raw31 = load_raw(w3[KP : 2 * KP, :], "tab1", "raw31")
+        load_page(6)
+        look(5)
+        less_ease(4, H_BYTES * 5)
+        xq = {}
+        for which in (1, 2):
+            codes, scales = quantise(xi[which, 0][0][:].rearrange("p m t -> p (m t)"), f"xq{which}0", H_BYTES * 5 + 1536 + 512 * which)
+            for hm in range(2):
+                xq[which, 0, hm] = (codes[:, HALF * hm : HALF * (hm + 1)], scales[:, HALF * hm : HALF * (hm + 1)])
+        g31 = group_w3(raw31, "g31")
+        scatter(6)
+
+        load_ease(5)
+        load_low(7)
+        load_ease(6)
+        load_page(7)
+        look(6)
+        less_ease(5, H_BYTES * 6)
+        floor_h(7)
+        less_ease(6, H_BYTES * 6 + 2048)
+        scatter(7)
+
+        load_ease(7)
+        w3q = [quantise(g30[:], "w3q0", H_BYTES * 7), quantise(g31[:], "w3q1", H_BYTES * 7 + 512)]
+
+        yacc = {}
+
+        def y_pass(which, b, hm):
+            codes, scales = xq[which, b, hm]
+            for pair in range(2):
+                if b == 0:
+                    yacc[which, hm, pair] = psum.tile([P, 2, HALF], F32, name=f"y{which}{hm}{pair}", tag=f"bank{4 * (which - 1) + 2 * hm + pair}")
+                for u in range(2):
+                    nt = 2 * pair + u
+                    if which == 1:
+                        w = w2w[:, b, 2 * P * nt : 2 * P * (nt + 1)].bitcast(FP4X4)
+                        ws = w2s[:, b, P * nt : P * (nt + 1)]
+                    else:
+                        w = w3q[b][0][:, P * nt : P * (nt + 1)].bitcast(FP8X4)
+                        ws = w3q[b][1][:, P * nt : P * (nt + 1)]
+                    nc.tensor.matmul_mx(out=yacc[which, hm, pair][:, u, :], lhsT=w, lhsT_scale=ws, rhs=codes.bitcast(FP8X4), rhs_scale=scales,
+                                        start=(b == 0 and u == 0), stop=(b == 1 and u == 1))
+
+        for which in (1, 2):
+            for hm in range(2):
+                y_pass(which, 0, hm)
+
+        look(7)
+        d7 = [keep.tile([P, HALF], F32, name=f"d7{hm}") for hm in range(2)]
+        for hm in range(2):
+            cols = slice(HALF * hm, HALF * (hm + 1))
+            nc.vector.tensor_tensor(out=d7[hm][:], in0=xs[7][:, cols], in1=eases[7][:, cols], op=ALU.subtract)
+        for hm in range(2):
+            nc.vector.tensor_scalar(out=xi[2, 1][hm][:, :, 3], in0=d7[hm][:], scalar1=col("gain2", 7), scalar2=None, op0=ALU.mult)
+        for hm in range(2):
+            for which in (2, 1):
+                codes, scales = quantise(xi[which, 1][hm][:].rearrange("p m t -> p (m t)"), f"xq{which}1{hm}")
+                xq[which, 1, hm] = (codes[:], scales[:])
+                y_pass(which, 1, hm)
+        for hm in range(2):
+            for pair in range(2):
+                res = keep.tile([P, 2, HALF], F32, name=f"res{hm}{pair}")
+                nc.scalar.copy(out=res[:], in_=yacc[2, hm, pair][:])
+                nc.vector.tensor_tensor(out=res[:], in0=yacc[1, hm, pair][:], in1=res[:], op=ALU.mult)
+                nc.sync.dma_start(out=out[2 * P * pair : 2 * P * (pair + 1), HALF * hm : HALF * (hm + 1)].rearrange("(u p) m -> p u m", u=2), in_=res[:])

@@ -1,6 +1,7 @@
 from contextlib import ExitStack
 
 import concourse.mybir as mybir
+from concourse.masks import make_identity
 
 K, T, S, H, T2, M, N = 1024, 2048, 1024, 1024, 2048, 512, 512
 FLOPS = 2 * K * H * S + 2 * 2 * H * N * M
@@ -22,6 +23,7 @@ KP = P * PACK
 BANK = 512
 HALF = M // 2
 H_BYTES = 4 * S
+H_AT = [H_BYTES - 64, 0] + [H_BYTES * i - 128 for i in range(2, 8)]
 
 
 def tile_list_tablature_fingering_kernel(tc, tab_words, tab_scales, offs, w1, low, page0, wgs, offs2, offs3,
@@ -32,34 +34,30 @@ def tile_list_tablature_fingering_kernel(tc, tab_words, tab_scales, offs, w1, lo
         ring = ctx.enter_context(tc.tile_pool(name="ring", bufs=4))
         bfp = ctx.enter_context(tc.tile_pool(name="bfp", bufs=2))
         hreg = ctx.enter_context(tc.tile_pool(name="hreg", bufs=1))
+        head = ctx.enter_context(tc.tile_pool(name="head", bufs=1))
         psum = ctx.enter_context(tc.psum_pool(name="psum", bufs=1))
 
         def rows(mat, i):
             b, t = divmod(i, PACK)
             return mat.rearrange("(b p t) c -> b t p c", b=2, t=PACK)[b, t]
 
-        tsc = keep.tile([P, T], U8, name="tsc", align_bytes=64)
+        ident = keep.tile([P, P], F32, name="ident")
+        make_identity(nc, ident[:])
+        tsc = head.tile([P, T], U8, name="tsc", align_bytes=64, offset=3072)
         nc.vector.memset(tsc[:].bitcast(U32), 0)
         for q in range(4):
             nc.scalar.dma_start(out=tsc[32 * q : 32 * q + 8, :].bitcast(I32), in_=tab_scales[:, 4 * q : 4 * q + 4, :].bitcast(I32))
         w2s = keep.tile([P, 2, N], U8, name="w2s", align_bytes=64)
-        nc.gpsimd.memset(w2s[:].rearrange("p a c -> p (a c)").bitcast(U32), 0)
-        for q in range(4):
-            nc.gpsimd.dma_start(out=w2s[32 * q : 32 * q + 4, :, :].bitcast(I32),
-                                in_=w2_scales[:, 4 * q : 4 * q + 4, :].rearrange("a r c -> r a c").bitcast(I32))
+        nc.vector.memset(w2s[:].rearrange("p a c -> p (a c)").bitcast(U32), 0)
         vec = {}
-        for name, v in (("cal_s", cal_s), ("cal_b", cal_b), ("gain1", gain1), ("gain2", gain2)):
+
+        def load_vec(name, v):
             vec[name] = keep.tile([P, 2, PACK], F32, name=name)
-            nc.gpsimd.dma_start(out=vec[name][:], in_=v.rearrange("(b p t) -> p b t", b=2, t=PACK))
+            nc.sync.dma_start(out=vec[name][:], in_=v.rearrange("(b p t) -> p b t", b=2, t=PACK))
 
         def col(name, i):
             b, t = divmod(i, PACK)
             return vec[name][:, b, t : t + 1]
-
-        wgs_q = wgs.rearrange("(q t) j -> q t j", t=PACK)
-        wg0 = keep.tile([P, S], F32, name="wg0")
-        for q in (0, 2, 1, 3):
-            nc.scalar.dma_start(out=wg0[32 * q : 32 * q + 32, :], in_=wgs_q[:, 0, :])
 
         def load_list(src, name):
             t = keep.tile([P, src.shape[1]], U16, name=name)
@@ -82,10 +80,7 @@ def tile_list_tablature_fingering_kernel(tc, tab_words, tab_scales, offs, w1, lo
         lows, pages, eases, hs, xs = {}, {}, {}, {}, {}
 
         def load_low(i):
-            if i == 0:
-                lows[i] = keep.tile([P, S], F32, name="low0", tag="low0")
-            else:
-                lows[i] = ring.tile([P, S], F32, name=f"low{i}", tag="low")
+            lows[i] = ring.tile([P, S], F32, name=f"low{i}", tag="low")
             nc.sync.dma_start(out=lows[i][:], in_=rows(low, i))
 
         def load_page(i):
@@ -96,9 +91,10 @@ def tile_list_tablature_fingering_kernel(tc, tab_words, tab_scales, offs, w1, lo
             eases[i] = keep.tile([P, M], F32, name=f"ease{i}")
             nc.sync.dma_start(out=eases[i][:], in_=rows(ease, i))
 
-        def group_w1(raw, name):
-            g = bfp.tile([P, 2048], BF16, name=name, tag="wbf", align_bytes=64)
-            nc.scalar.copy(out=g[:].rearrange("p (t m j) -> p m j t", t=PACK, j=PACK),
+        def group_w1(raw, name, copy, g=None):
+            if g is None:
+                g = bfp.tile([P, 2048], BF16, name=name, tag="wbf", align_bytes=64)
+            copy(out=g[:].rearrange("p (t m j) -> p m j t", t=PACK, j=PACK),
                            in_=raw[:].rearrange("p j (m t) -> p m j t", t=PACK))
             return g
 
@@ -120,6 +116,8 @@ def tile_list_tablature_fingering_kernel(tc, tab_words, tab_scales, offs, w1, lo
 
         o1 = load_list(offs, "o1")
         tab0 = load_tab(0)
+        wnat = keep.tile([P, S], F32, name="wnat")
+        nc.sync.dma_start(out=wnat[:], in_=wgs)
         raw00 = load_raw(w1_part(0, 0), "raw0", "raw00")
         raw10 = load_raw(w1_part(1, 0), "raw1", "raw10")
         tab1 = load_tab(1)
@@ -129,38 +127,57 @@ def tile_list_tablature_fingering_kernel(tc, tab_words, tab_scales, offs, w1, lo
 
         gw = {}
 
-        def gather_words(tab, a, hj):
-            gw[a, hj] = keep.tile([P, BANK], U32, name=f"gw{a}{hj}", align_bytes=64)
-            nc.vector.tensor_copy(out=gw[a, hj][:], in_=tab[:].bitcast(U32).indirect(o1[:, 32 * hj : 32 * hj + 32]))
+        def gather_words(tab, a, picked):
+            for hj in range(2):
+                gw[a, hj] = picked[:, BANK * hj : BANK * (hj + 1)]
+                nc.vector.tensor_copy(out=gw[a, hj], in_=tab[:].bitcast(U32).indirect(o1[:, 32 * hj : 32 * hj + 32]))
 
-        gather_words(tab0, 0, 0)
-        gather_words(tab0, 0, 1)
+        gather_words(tab0, 0, keep.tile([P, S], U32, name="gw0", align_bytes=64))
         gs = keep.tile([P, S], U8, name="gs", align_bytes=64)
         nc.vector.tensor_copy(out=gs[:], in_=tsc[:].indirect(o1[:]))
         w1q = {}
-        g00 = group_w1(raw00, "g00")
-        g10 = group_w1(raw10, "g10")
+        g00 = group_w1(raw00, "g00", nc.scalar.copy)
+        g10 = group_w1(raw10, "g10", nc.vector.tensor_copy, head.tile([P, 2048], BF16, name="g10", align_bytes=64, offset=0))
         w1q[0, 0] = quantise(g00[:], "w1q00")
-        gather_words(tab1, 1, 0)
         w1q[1, 0] = quantise(g10[:], "w1q10")
-        gather_words(tab1, 1, 1)
+        gather_words(tab1, 1, head.tile([P, S], U32, name="gw1", align_bytes=64, offset=4096))
+
+        turned = []
+        for hj in range(2):
+            bank = psum.tile([P, 4, P], F32, name=f"turned{hj}", tag=f"bank{4 + hj}")
+            for c in range(4):
+                nc.tensor.transpose(bank[:, c, :], wnat[:, BANK * hj + P * c : BANK * hj + P * (c + 1)], ident[:])
+            turned.append(bank)
+        wg = {}
+
+        def deal_wgs(t):
+            wg[t] = keep.tile([P, S], F32, name=f"wg{t}")
+            staged = []
+            for hj in range(2):
+                st = keep.tile([P, 4, 4, 32], F32, name=f"staged{t}{hj}", tag=f"staged{hj}")
+                picked = turned[hj][:].rearrange("p c (q t) -> p c t q", t=PACK)[:, :, t : t + 1, :]
+                nc.scalar.copy(out=st[:], in_=picked.to_broadcast([P, 4, 4, 32]))
+                staged.append(st)
+            for hj in range(2):
+                back = psum.tile([P, 4, P], F32, name=f"back{t}{hj}", tag=f"bank{6 + hj}")
+                for c in range(4):
+                    nc.tensor.transpose(back[:, c, :], staged[hj][:, c, :, :].rearrange("p d q -> p (d q)"), ident[:])
+                nc.scalar.copy(out=wg[t][:, BANK * hj : BANK * (hj + 1)], in_=back[:].rearrange("p c j -> p (c j)"))
 
         def floor_h(i):
             b, t = divmod(i, PACK)
-            hs[i] = hreg.tile([P, S], F32, name=f"h{i}", align_bytes=64, offset=H_BYTES * i)
+            hs[i] = hreg.tile([P, S], F32, name=f"h{i}", align_bytes=64, offset=H_AT[i])
             for hj in range(2):
                 cols = slice(BANK * hj, BANK * (hj + 1))
-                acc = psum.tile([P, BANK], F32, name=f"hacc{i}_{hj}", tag=f"bank{2 * (i % 4) + hj}")
+                acc = psum.tile([P, BANK], F32, name=f"hacc{i}_{hj}", tag=f"bank{2 * (i % 2) + hj}")
                 for a in range(2):
                     codes, scales = w1q[a, b]
                     nc.tensor.matmul_mx(out=acc[:], lhsT=codes[:, P * t : P * (t + 1)].bitcast(FP8X4), lhsT_scale=scales[:, P * t : P * (t + 1)],
-                                        rhs=gw[a, hj][:].bitcast(FP8X4), rhs_scale=gs[4 * a : P, cols], start=(a == 0), stop=(a == 1))
+                                        rhs=gw[a, hj].bitcast(FP8X4), rhs_scale=gs[4 * a : P, cols], start=(a == 0), stop=(a == 1))
                 nc.vector.tensor_tensor(out=hs[i][:, cols], in0=acc[:], in1=lows[i][:, cols], op=ALU.max)
 
-        wg = {0: wg0[:]}
-
         def scatter(i):
-            nc.vector.tensor_tensor(out=pages[i][:].indirect(o2[:]), in0=hs[i][:], in1=wg[i % PACK], op=ALU.mult)
+            nc.vector.tensor_tensor(out=pages[i][:].indirect(o2[:]), in0=hs[i][:], in1=wg[i % PACK][:], op=ALU.mult)
 
         xi = {}
         for which in (1, 2):
@@ -184,13 +201,11 @@ def tile_list_tablature_fingering_kernel(tc, tab_words, tab_scales, offs, w1, lo
             nc.vector.tensor_tensor(out=d[:], in0=xs[i][:], in1=eases[i][:], op=ALU.subtract)
             plane(2, i, d)
 
+        deal_wgs(0)
         floor_h(0)
         scatter(0)
-        wg123 = keep.tile([P, 3, S], F32, name="wg123", tag="low0")
-        for q in (0, 2, 1, 3):
-            nc.scalar.dma_start(out=wg123[32 * q : 32 * q + 32, :, :], in_=wgs_q[:, 1:PACK, :])
         for t in range(1, PACK):
-            wg[t] = wg123[:, t - 1, :]
+            deal_wgs(t)
 
         load_low(1)
         load_low(2)
@@ -202,10 +217,14 @@ def tile_list_tablature_fingering_kernel(tc, tab_words, tab_scales, offs, w1, lo
         raw01 = load_raw(w1_part(0, 1), "raw1", "raw01")
         raw11 = load_raw(w1_part(1, 1), "raw0", "raw11")
         o3 = load_list(offs3, "o3")
+        load_vec("cal_s", cal_s)
+        load_vec("cal_b", cal_b)
         load_low(3)
+        load_vec("gain1", gain1)
         load_page(2)
-        g01 = group_w1(raw01, "g01")
-        g11 = group_w1(raw11, "g11")
+        load_vec("gain2", gain2)
+        g01 = group_w1(raw01, "g01", nc.scalar.copy)
+        g11 = group_w1(raw11, "g11", nc.scalar.copy)
         look(0)
         look(1)
         floor_h(3)
@@ -214,11 +233,11 @@ def tile_list_tablature_fingering_kernel(tc, tab_words, tab_scales, offs, w1, lo
         load_ease(0)
         load_ease(1)
         load_page(3)
-        w1q[0, 1] = quantise(g01[:], "w1q01", H_BYTES * 2 + 2048)
-        w1q[1, 1] = quantise(g11[:], "w1q11", H_BYTES * 2 + 2560)
+        w1q[0, 1] = quantise(g01[:], "w1q01", H_AT[2] + 2048)
+        w1q[1, 1] = quantise(g11[:], "w1q11", H_AT[2] + 2560)
         look(2)
-        less_ease(0, H_BYTES * 1)
-        less_ease(1, H_BYTES * 2)
+        less_ease(0, H_AT[1])
+        less_ease(1, H_AT[2])
         scatter(3)
 
         load_ease(2)
@@ -226,7 +245,7 @@ def tile_list_tablature_fingering_kernel(tc, tab_words, tab_scales, offs, w1, lo
         load_low(5)
         load_page(4)
         look(3)
-        less_ease(2, H_BYTES * 3)
+        less_ease(2, H_AT[3])
         floor_h(4)
         floor_h(5)
         scatter(4)
@@ -237,8 +256,11 @@ def tile_list_tablature_fingering_kernel(tc, tab_words, tab_scales, offs, w1, lo
         w2w = keep.tile([P, 2, 2 * N], U8, name="w2w", align_bytes=64)
         nc.sync.dma_start(out=w2w[:].bitcast(I32), in_=w2_words.rearrange("a p c -> p a c").bitcast(I32))
         load_page(5)
+        for q in range(4):
+            nc.sync.dma_start(out=w2s[32 * q : 32 * q + 4, :, :].bitcast(I32),
+                              in_=w2_scales[:, 4 * q : 4 * q + 4, :].rearrange("a r c -> r a c").bitcast(I32))
         look(4)
-        less_ease(3, H_BYTES * 4)
+        less_ease(3, H_AT[4])
         floor_h(6)
         g30 = group_w3(raw30, "g30")
         scatter(5)
@@ -247,10 +269,10 @@ def tile_list_tablature_fingering_kernel(tc, tab_words, tab_scales, offs, w1, lo
         raw31 = load_raw(w3[KP : 2 * KP, :], "tab1", "raw31")
         load_page(6)
         look(5)
-        less_ease(4, H_BYTES * 5)
+        less_ease(4, H_AT[5])
         xq = {}
         for which in (1, 2):
-            codes, scales = quantise(xi[which, 0][0][:].rearrange("p m t -> p (m t)"), f"xq{which}0", H_BYTES * 5 + 1536 + 512 * which)
+            codes, scales = quantise(xi[which, 0][0][:].rearrange("p m t -> p (m t)"), f"xq{which}0", H_AT[5] + 1536 + 512 * which)
             for hm in range(2):
                 xq[which, 0, hm] = (codes[:, HALF * hm : HALF * (hm + 1)], scales[:, HALF * hm : HALF * (hm + 1)])
         g31 = group_w3(raw31, "g31")
@@ -261,13 +283,13 @@ def tile_list_tablature_fingering_kernel(tc, tab_words, tab_scales, offs, w1, lo
         load_ease(6)
         load_page(7)
         look(6)
-        less_ease(5, H_BYTES * 6)
+        less_ease(5, H_AT[6])
         floor_h(7)
-        less_ease(6, H_BYTES * 6 + 2048)
+        less_ease(6, H_AT[6] + 2048)
         scatter(7)
 
         load_ease(7)
-        w3q = [quantise(g30[:], "w3q0", H_BYTES * 7), quantise(g31[:], "w3q1", H_BYTES * 7 + 512)]
+        w3q = [quantise(g30[:], "w3q0", H_AT[7]), quantise(g31[:], "w3q1", H_AT[7] + 512)]
 
         yacc = {}
 
@@ -275,7 +297,7 @@ def tile_list_tablature_fingering_kernel(tc, tab_words, tab_scales, offs, w1, lo
             codes, scales = xq[which, b, hm]
             for pair in range(2):
                 if b == 0:
-                    yacc[which, hm, pair] = psum.tile([P, 2, HALF], F32, name=f"y{which}{hm}{pair}", tag=f"bank{4 * (which - 1) + 2 * hm + pair}")
+                    yacc[which, hm, pair] = psum.tile([P, 2, HALF], F32, name=f"y{which}{hm}{pair}", tag=f"bank{4 * (2 - which) + 2 * hm + pair}")
                 for u in range(2):
                     nt = 2 * pair + u
                     if which == 1:

@@ -23,7 +23,9 @@ KP = P * PACK
 BANK = 512
 HALF = M // 2
 H_BYTES = 4 * S
-H_AT = [H_BYTES - 64, 0] + [H_BYTES * i - 128 for i in range(2, 8)]
+H_STEP = H_BYTES - 64
+H_AT = [H_STEP * (4 + i // 2 if i % 2 == 0 else 3 - i // 2) for i in range(8)]
+D_AT, PLANE_AT = 128, (2176, 2688)
 
 
 def tile_list_tablature_fingering_kernel(tc, tab_words, tab_scales, offs, w1, low, page0, wgs, offs2, offs3,
@@ -79,9 +81,10 @@ def tile_list_tablature_fingering_kernel(tc, tab_words, tab_scales, offs, w1, lo
 
         lows, pages, eases, hs, xs = {}, {}, {}, {}, {}
 
-        def load_low(i):
-            lows[i] = ring.tile([P, S], F32, name=f"low{i}", tag="low")
-            nc.sync.dma_start(out=lows[i][:], in_=rows(low, i))
+        def load_low(i, cols=slice(0, S)):
+            if i not in lows:
+                lows[i] = ring.tile([P, S], F32, name=f"low{i}", tag="low")
+            nc.sync.dma_start(out=lows[i][:, cols], in_=rows(low, i)[:, cols])
 
         def load_page(i):
             pages[i] = ring.tile([P, T2], F32, name=f"page{i}", tag="page")
@@ -91,12 +94,16 @@ def tile_list_tablature_fingering_kernel(tc, tab_words, tab_scales, offs, w1, lo
             eases[i] = keep.tile([P, M], F32, name=f"ease{i}")
             nc.sync.dma_start(out=eases[i][:], in_=rows(ease, i))
 
-        def group_w1(raw, name, copy, g=None):
-            if g is None:
-                g = bfp.tile([P, 2048], BF16, name=name, tag="wbf", align_bytes=64)
-            copy(out=g[:].rearrange("p (t m j) -> p m j t", t=PACK, j=PACK),
-                           in_=raw[:].rearrange("p j (m t) -> p m j t", t=PACK))
+        def group_w1(raw, g, shares):
+            for copy, ms in shares:
+                copy(out=g[:].rearrange("p (t m j) -> p m j t", t=PACK, j=PACK)[:, ms, :, :],
+                     in_=raw[:].rearrange("p j (m t) -> p m j t", t=PACK)[:, ms, :, :])
             return g
+
+        def wbf(name):
+            return bfp.tile([P, 2048], BF16, name=name, tag="wbf", align_bytes=64)
+
+        on_scalar = [(nc.scalar.copy, slice(0, P))]
 
         def group_w3(raw, name):
             g = bfp.tile([P, 2048], BF16, name=name, tag="wbf", align_bytes=64)
@@ -116,14 +123,15 @@ def tile_list_tablature_fingering_kernel(tc, tab_words, tab_scales, offs, w1, lo
 
         o1 = load_list(offs, "o1")
         tab0 = load_tab(0)
-        wnat = keep.tile([P, S], F32, name="wnat")
+        wnat = head.tile([P, S], F32, name="wnat", align_bytes=64, offset=8192)
         nc.sync.dma_start(out=wnat[:], in_=wgs)
         raw00 = load_raw(w1_part(0, 0), "raw0", "raw00")
         raw10 = load_raw(w1_part(1, 0), "raw1", "raw10")
         tab1 = load_tab(1)
         o2 = load_list(offs2, "o2")
-        load_low(0)
+        load_low(0, slice(0, BANK))
         load_page(0)
+        load_low(0, slice(BANK, S))
 
         gw = {}
 
@@ -136,8 +144,9 @@ def tile_list_tablature_fingering_kernel(tc, tab_words, tab_scales, offs, w1, lo
         gs = keep.tile([P, S], U8, name="gs", align_bytes=64)
         nc.vector.tensor_copy(out=gs[:], in_=tsc[:].indirect(o1[:]))
         w1q = {}
-        g00 = group_w1(raw00, "g00", nc.scalar.copy)
-        g10 = group_w1(raw10, "g10", nc.vector.tensor_copy, head.tile([P, 2048], BF16, name="g10", align_bytes=64, offset=0))
+        g00 = group_w1(raw00, wbf("g00"), on_scalar)
+        g10 = head.tile([P, 2048], BF16, name="g10", align_bytes=64, offset=0)
+        group_w1(raw10, g10, [(nc.vector.tensor_copy, slice(0, P))])
         w1q[0, 0] = quantise(g00[:], "w1q00")
         w1q[1, 0] = quantise(g10[:], "w1q10")
         gather_words(tab1, 1, head.tile([P, S], U32, name="gw1", align_bytes=64, offset=4096))
@@ -154,30 +163,32 @@ def tile_list_tablature_fingering_kernel(tc, tab_words, tab_scales, offs, w1, lo
             wg[t] = keep.tile([P, S], F32, name=f"wg{t}")
             staged = []
             for hj in range(2):
-                st = keep.tile([P, 4, 4, 32], F32, name=f"staged{t}{hj}", tag=f"staged{hj}")
+                st = head.tile([P, 4, 4, 32], F32, name=f"staged{t}{hj}", align_bytes=64, offset=(12288, 12288, 8192, 12288)[t] + 2048 * hj)
                 picked = turned[hj][:].rearrange("p c (q t) -> p c t q", t=PACK)[:, :, t : t + 1, :]
                 nc.scalar.copy(out=st[:], in_=picked.to_broadcast([P, 4, 4, 32]))
                 staged.append(st)
             for hj in range(2):
-                back = psum.tile([P, 4, P], F32, name=f"back{t}{hj}", tag=f"bank{6 + hj}")
+                back = psum.tile([P, 4, P], F32, name=f"back{t}{hj}", tag=f"bank{(0, 2, 6, 6)[t] + hj}")
                 for c in range(4):
                     nc.tensor.transpose(back[:, c, :], staged[hj][:, c, :, :].rearrange("p d q -> p (d q)"), ident[:])
                 nc.scalar.copy(out=wg[t][:, BANK * hj : BANK * (hj + 1)], in_=back[:].rearrange("p c j -> p (c j)"))
 
-        def floor_h(i):
+        def floor_h(i, halves=(0, 1)):
             b, t = divmod(i, PACK)
-            hs[i] = hreg.tile([P, S], F32, name=f"h{i}", align_bytes=64, offset=H_AT[i])
-            for hj in range(2):
+            if i not in hs:
+                hs[i] = hreg.tile([P, S], F32, name=f"h{i}", align_bytes=64, offset=H_AT[i])
+            for hj in halves:
                 cols = slice(BANK * hj, BANK * (hj + 1))
-                acc = psum.tile([P, BANK], F32, name=f"hacc{i}_{hj}", tag=f"bank{2 * (i % 2) + hj}")
+                acc = psum.tile([P, BANK], F32, name=f"hacc{i}_{hj}", tag=f"bank{2 * (i % 4) + hj}")
                 for a in range(2):
                     codes, scales = w1q[a, b]
                     nc.tensor.matmul_mx(out=acc[:], lhsT=codes[:, P * t : P * (t + 1)].bitcast(FP8X4), lhsT_scale=scales[:, P * t : P * (t + 1)],
                                         rhs=gw[a, hj].bitcast(FP8X4), rhs_scale=gs[4 * a : P, cols], start=(a == 0), stop=(a == 1))
                 nc.vector.tensor_tensor(out=hs[i][:, cols], in0=acc[:], in1=lows[i][:, cols], op=ALU.max)
 
-        def scatter(i):
-            nc.vector.tensor_tensor(out=pages[i][:].indirect(o2[:]), in0=hs[i][:], in1=wg[i % PACK][:], op=ALU.mult)
+        def scatter(i, first=0, last=S):
+            nc.vector.tensor_tensor(out=pages[i][:].indirect(o2[:, first // 16 : last // 16]), in0=hs[i][:, first:last],
+                                    in1=wg[i % PACK][:, first:last], op=ALU.mult)
 
         xi = {}
         for which in (1, 2):
@@ -196,14 +207,18 @@ def tile_list_tablature_fingering_kernel(tc, tab_words, tab_scales, offs, w1, lo
             nc.scalar.activation(out=xs[i][:], in_=pages[i][:].indirect(o3[:]), func=ACT.Sigmoid, bias=col("cal_b", i), scale=col("cal_s", i))
             plane(1, i, xs[i])
 
-        def less_ease(i, offset):
-            d = hreg.tile([P, M], F32, name=f"d{i}", align_bytes=64, offset=offset)
-            nc.vector.tensor_tensor(out=d[:], in0=xs[i][:], in1=eases[i][:], op=ALU.subtract)
+        def less_ease(i, engine):
+            if i < 6:
+                d = hreg.tile([P, M], F32, name=f"d{i}", align_bytes=64, offset=H_AT[i + 1] + D_AT)
+            else:
+                d = keep.tile([P, M], F32, name=f"d{i}")
+            engine.tensor_tensor(out=d[:], in0=xs[i][:], in1=eases[i][:], op=ALU.subtract)
             plane(2, i, d)
 
         deal_wgs(0)
-        floor_h(0)
-        scatter(0)
+        for hj in range(2):
+            floor_h(0, (hj,))
+            scatter(0, BANK * hj, BANK * (hj + 1))
         for t in range(1, PACK):
             deal_wgs(t)
 
@@ -221,37 +236,37 @@ def tile_list_tablature_fingering_kernel(tc, tab_words, tab_scales, offs, w1, lo
         load_vec("cal_b", cal_b)
         load_low(3)
         load_vec("gain1", gain1)
-        load_page(2)
+        load_ease(0)
         load_vec("gain2", gain2)
-        g01 = group_w1(raw01, "g01", nc.scalar.copy)
-        g11 = group_w1(raw11, "g11", nc.scalar.copy)
+        load_page(2)
+        g01 = group_w1(raw01, wbf("g01"), on_scalar)
+        g11 = group_w1(raw11, wbf("g11"), on_scalar)
         look(0)
         look(1)
         floor_h(3)
+        less_ease(0, nc.gpsimd)
+        w1q[0, 1] = quantise(g01[:], "w1q01", H_AT[1] + PLANE_AT[0])
+        w1q[1, 1] = quantise(g11[:], "w1q11", H_AT[1] + PLANE_AT[1])
         scatter(2)
 
-        load_ease(0)
+        load_low(4)
         load_ease(1)
         load_page(3)
-        w1q[0, 1] = quantise(g01[:], "w1q01", H_AT[2] + 2048)
-        w1q[1, 1] = quantise(g11[:], "w1q11", H_AT[2] + 2560)
         look(2)
-        less_ease(0, H_AT[1])
-        less_ease(1, H_AT[2])
+        floor_h(4)
+        less_ease(1, nc.gpsimd)
         scatter(3)
 
-        load_ease(2)
-        load_low(4)
         load_low(5)
+        load_ease(2)
         load_page(4)
         look(3)
-        less_ease(2, H_AT[3])
-        floor_h(4)
         floor_h(5)
+        less_ease(2, nc.gpsimd)
         scatter(4)
 
-        load_ease(3)
         load_low(6)
+        load_ease(3)
         raw30 = load_raw(w3[0:KP, :], "tab0", "raw30")
         w2w = keep.tile([P, 2, 2 * N], U8, name="w2w", align_bytes=64)
         nc.sync.dma_start(out=w2w[:].bitcast(I32), in_=w2_words.rearrange("a p c -> p a c").bitcast(I32))
@@ -260,36 +275,36 @@ def tile_list_tablature_fingering_kernel(tc, tab_words, tab_scales, offs, w1, lo
             nc.sync.dma_start(out=w2s[32 * q : 32 * q + 4, :, :].bitcast(I32),
                               in_=w2_scales[:, 4 * q : 4 * q + 4, :].rearrange("a r c -> r a c").bitcast(I32))
         look(4)
-        less_ease(3, H_AT[4])
         floor_h(6)
+        less_ease(3, nc.gpsimd)
         g30 = group_w3(raw30, "g30")
         scatter(5)
 
+        load_low(7)
         load_ease(4)
         raw31 = load_raw(w3[KP : 2 * KP, :], "tab1", "raw31")
         load_page(6)
         look(5)
-        less_ease(4, H_AT[5])
-        xq = {}
-        for which in (1, 2):
-            codes, scales = quantise(xi[which, 0][0][:].rearrange("p m t -> p (m t)"), f"xq{which}0", H_AT[5] + 1536 + 512 * which)
-            for hm in range(2):
-                xq[which, 0, hm] = (codes[:, HALF * hm : HALF * (hm + 1)], scales[:, HALF * hm : HALF * (hm + 1)])
+        floor_h(7)
+        less_ease(4, nc.gpsimd)
         g31 = group_w3(raw31, "g31")
         scatter(6)
 
         load_ease(5)
-        load_low(7)
         load_ease(6)
         load_page(7)
         look(6)
-        less_ease(5, H_AT[6])
-        floor_h(7)
-        less_ease(6, H_AT[6] + 2048)
+        less_ease(5, nc.vector)
+        xq = {}
+        for which in (1, 2):
+            codes, scales = quantise(xi[which, 0][0][:].rearrange("p m t -> p (m t)"), f"xq{which}0", H_AT[6] + PLANE_AT[which - 1])
+            for hm in range(2):
+                xq[which, 0, hm] = (codes[:, HALF * hm : HALF * (hm + 1)], scales[:, HALF * hm : HALF * (hm + 1)])
+        less_ease(6, nc.vector)
         scatter(7)
 
         load_ease(7)
-        w3q = [quantise(g30[:], "w3q0", H_AT[7]), quantise(g31[:], "w3q1", H_AT[7] + 512)]
+        w3q = [quantise(g30[:], "w3q0", H_AT[7] + PLANE_AT[0]), quantise(g31[:], "w3q1", H_AT[7] + PLANE_AT[1])]
 
         yacc = {}
 
@@ -297,7 +312,7 @@ def tile_list_tablature_fingering_kernel(tc, tab_words, tab_scales, offs, w1, lo
             codes, scales = xq[which, b, hm]
             for pair in range(2):
                 if b == 0:
-                    yacc[which, hm, pair] = psum.tile([P, 2, HALF], F32, name=f"y{which}{hm}{pair}", tag=f"bank{4 * (2 - which) + 2 * hm + pair}")
+                    yacc[which, hm, pair] = psum.tile([P, 2, HALF], F32, name=f"y{which}{hm}{pair}", tag=f"bank{4 * (which - 1) + 2 * hm + pair}")
                 for u in range(2):
                     nt = 2 * pair + u
                     if which == 1:
@@ -329,5 +344,8 @@ def tile_list_tablature_fingering_kernel(tc, tab_words, tab_scales, offs, w1, lo
             for pair in range(2):
                 res = keep.tile([P, 2, HALF], F32, name=f"res{hm}{pair}")
                 nc.scalar.copy(out=res[:], in_=yacc[2, hm, pair][:])
-                nc.vector.tensor_tensor(out=res[:], in0=yacc[1, hm, pair][:], in1=res[:], op=ALU.mult)
-                nc.sync.dma_start(out=out[2 * P * pair : 2 * P * (pair + 1), HALF * hm : HALF * (hm + 1)].rearrange("(u p) m -> p u m", u=2), in_=res[:])
+                dst = out[2 * P * pair : 2 * P * (pair + 1), HALF * hm : HALF * (hm + 1)].rearrange("(u p) m -> p u m", u=2)
+                pieces = [slice(0, 1), slice(1, 2)] if (hm, pair) == (1, 1) else [slice(0, 2)]
+                for n, u in enumerate(pieces):
+                    nc.vector.tensor_tensor(out=res[:, u, :], in0=yacc[1, hm, pair][:, u, :], in1=res[:, u, :], op=ALU.mult)
+                    (nc.sync, nc.scalar)[n].dma_start(out=dst[:, u, :], in_=res[:, u, :])

@@ -20,12 +20,17 @@ ALU = mybir.AluOpType
 P = 128
 PACK = 4
 KP = P * PACK
+TILES = H // P
 BANK = 512
+LIST_HALF = BANK // 16
 HALF = M // 2
-H_BYTES = 4 * S
-H_STEP = H_BYTES - 64
-H_AT = [H_STEP * (4 + i // 2 if i % 2 == 0 else 3 - i // 2) for i in range(8)]
-D_AT, PLANE_AT = 128, (2176, 2688)
+W3_STEP = 5
+
+H_STEP = 4 * S - 64
+H_AT = [H_STEP * (4 + i // 2 if i % 2 == 0 else 3 - i // 2) for i in range(TILES)]
+PLANE_AT = (2176, 2688)
+
+W1_GROUPED_AT, TAB_SCALES_AT, WORDS1_AT, WGS_AT, STAGE_AT = 0, 3072, 4096, 8192, 12288
 
 
 def tile_list_tablature_fingering_kernel(tc, tab_words, tab_scales, offs, w1, low, page0, wgs, offs2, offs3,
@@ -39,47 +44,37 @@ def tile_list_tablature_fingering_kernel(tc, tab_words, tab_scales, offs, w1, lo
         head = ctx.enter_context(tc.tile_pool(name="head", bufs=1))
         psum = ctx.enter_context(tc.psum_pool(name="psum", bufs=1))
 
+        lows, pages, eases, hs, xs, vec, words, wg, w1q, xq, yacc = {}, {}, {}, {}, {}, {}, {}, {}, {}, {}, {}
+
         def rows(mat, i):
             b, t = divmod(i, PACK)
             return mat.rearrange("(b p t) c -> b t p c", b=2, t=PACK)[b, t]
-
-        ident = keep.tile([P, P], F32, name="ident")
-        make_identity(nc, ident[:])
-        tsc = head.tile([P, T], U8, name="tsc", align_bytes=64, offset=3072)
-        nc.vector.memset(tsc[:].bitcast(U32), 0)
-        for q in range(4):
-            nc.scalar.dma_start(out=tsc[32 * q : 32 * q + 8, :].bitcast(I32), in_=tab_scales[:, 4 * q : 4 * q + 4, :].bitcast(I32))
-        w2s = keep.tile([P, 2, N], U8, name="w2s", align_bytes=64)
-        nc.vector.memset(w2s[:].rearrange("p a c -> p (a c)").bitcast(U32), 0)
-        vec = {}
-
-        def load_vec(name, v):
-            vec[name] = keep.tile([P, 2, PACK], F32, name=name)
-            nc.sync.dma_start(out=vec[name][:], in_=v.rearrange("(b p t) -> p b t", b=2, t=PACK))
 
         def col(name, i):
             b, t = divmod(i, PACK)
             return vec[name][:, b, t : t + 1]
 
+        def load_vec(name, src):
+            vec[name] = keep.tile([P, 2, PACK], F32, name=name)
+            nc.sync.dma_start(out=vec[name][:], in_=src.rearrange("(b p t) -> p b t", b=2, t=PACK))
+
         def load_list(src, name):
-            t = keep.tile([P, src.shape[1]], U16, name=name)
-            nc.sync.dma_start(t[:], src)
-            return t
+            tile = keep.tile([P, src.shape[1]], U16, name=name)
+            nc.sync.dma_start(tile[:], src)
+            return tile
 
         def load_tab(a):
-            t = keep.tile([P, T], I32, name=f"tabw{a}", tag=f"tab{a}")
-            nc.sync.dma_start(out=t[:], in_=tab_words[a].rearrange("p t i -> p (t i)").bitcast(I32))
-            return t
+            tile = keep.tile([P, T], I32, name=f"tabw{a}", tag=f"tab{a}")
+            nc.sync.dma_start(out=tile[:], in_=tab_words[a].rearrange("p t i -> p (t i)").bitcast(I32))
+            return tile
 
         def load_raw(src, tag, name):
-            t = keep.tile([P, PACK, 512], F32, name=name, tag=tag)
-            nc.sync.dma_start(out=t[:], in_=src.rearrange("(p j) c -> p j c", j=PACK))
-            return t
+            tile = keep.tile([P, PACK, KP], F32, name=name, tag=tag)
+            nc.sync.dma_start(out=tile[:], in_=src.rearrange("(p j) c -> p j c", j=PACK))
+            return tile
 
         def w1_part(a, b):
             return w1[KP * a : KP * (a + 1), KP * b : KP * (b + 1)]
-
-        lows, pages, eases, hs, xs = {}, {}, {}, {}, {}
 
         def load_low(i, cols=slice(0, S)):
             if i not in lows:
@@ -94,219 +89,88 @@ def tile_list_tablature_fingering_kernel(tc, tab_words, tab_scales, offs, w1, lo
             eases[i] = keep.tile([P, M], F32, name=f"ease{i}")
             nc.sync.dma_start(out=eases[i][:], in_=rows(ease, i))
 
-        def group_w1(raw, g, shares):
-            for copy, ms in shares:
-                copy(out=g[:].rearrange("p (t m j) -> p m j t", t=PACK, j=PACK)[:, ms, :, :],
-                     in_=raw[:].rearrange("p j (m t) -> p m j t", t=PACK)[:, ms, :, :])
-            return g
+        def grouped_tile(name):
+            return bfp.tile([P, PACK * KP], BF16, name=name, tag="wbf", align_bytes=64)
 
-        def wbf(name):
-            return bfp.tile([P, 2048], BF16, name=name, tag="wbf", align_bytes=64)
-
-        on_scalar = [(nc.scalar.copy, slice(0, P))]
+        def group_w1(raw, grouped, copy):
+            copy(out=grouped[:].rearrange("p (t m j) -> p m j t", t=PACK, j=PACK),
+                 in_=raw[:].rearrange("p j (m t) -> p m j t", t=PACK))
+            return grouped
 
         def group_w3(raw, name):
-            g = bfp.tile([P, 2048], BF16, name=name, tag="wbf", align_bytes=64)
-            nc.scalar.copy(out=g[:].rearrange("p (c i j) -> p c j i", i=4, j=PACK),
-                           in_=raw[:].rearrange("p j (c i) -> p c j i", i=4))
-            return g
+            grouped = grouped_tile(name)
+            nc.scalar.copy(out=grouped[:].rearrange("p (c n j) -> p c j n", n=4, j=PACK),
+                           in_=raw[:].rearrange("p j (c n) -> p c j n", n=4))
+            return grouped
 
-        def quantise(grouped, name, offset=None):
+        def quantise(grouped, name, plane_at=None):
             width = grouped.shape[1] // PACK
             codes = keep.tile([P, width], U32, name=name + "_codes", align_bytes=64)
-            if offset is None:
+            if plane_at is None:
                 scales = keep.tile([P, width], U8, name=name + "_scales", align_bytes=64)
             else:
-                scales = hreg.tile([P, width], U8, name=name + "_scales", align_bytes=64, offset=offset)
+                scales = hreg.tile([P, width], U8, name=name + "_scales", align_bytes=64, offset=plane_at)
             nc.vector.quantize_mx(out=codes[:].bitcast(FP8X4), scales=scales[:], in_=grouped)
             return codes, scales
 
-        o1 = load_list(offs, "o1")
-        tab0 = load_tab(0)
-        wnat = head.tile([P, S], F32, name="wnat", align_bytes=64, offset=8192)
-        nc.sync.dma_start(out=wnat[:], in_=wgs)
-        raw00 = load_raw(w1_part(0, 0), "raw0", "raw00")
-        raw10 = load_raw(w1_part(1, 0), "raw1", "raw10")
-        tab1 = load_tab(1)
-        o2 = load_list(offs2, "o2")
-        load_low(0, slice(0, BANK))
-        load_page(0)
-        load_low(0, slice(BANK, S))
-
-        gw = {}
-
         def gather_words(tab, a, picked):
             for hj in range(2):
-                gw[a, hj] = picked[:, BANK * hj : BANK * (hj + 1)]
-                nc.vector.tensor_copy(out=gw[a, hj], in_=tab[:].bitcast(U32).indirect(o1[:, 32 * hj : 32 * hj + 32]))
-
-        gather_words(tab0, 0, keep.tile([P, S], U32, name="gw0", align_bytes=64))
-        gs = keep.tile([P, S], U8, name="gs", align_bytes=64)
-        nc.vector.tensor_copy(out=gs[:], in_=tsc[:].indirect(o1[:]))
-        w1q = {}
-        g00 = group_w1(raw00, wbf("g00"), on_scalar)
-        g10 = head.tile([P, 2048], BF16, name="g10", align_bytes=64, offset=0)
-        group_w1(raw10, g10, [(nc.vector.tensor_copy, slice(0, P))])
-        w1q[0, 0] = quantise(g00[:], "w1q00")
-        w1q[1, 0] = quantise(g10[:], "w1q10")
-        gather_words(tab1, 1, head.tile([P, S], U32, name="gw1", align_bytes=64, offset=4096))
-
-        turned = []
-        for hj in range(2):
-            bank = psum.tile([P, 4, P], F32, name=f"turned{hj}", tag=f"bank{4 + hj}")
-            for c in range(4):
-                nc.tensor.transpose(bank[:, c, :], wnat[:, BANK * hj + P * c : BANK * hj + P * (c + 1)], ident[:])
-            turned.append(bank)
-        wg = {}
+                words[a, hj] = picked[:, BANK * hj : BANK * (hj + 1)]
+                nc.vector.tensor_copy(out=words[a, hj], in_=tab[:].bitcast(U32).indirect(list1[:, LIST_HALF * hj : LIST_HALF * (hj + 1)]))
 
         def deal_wgs(t):
             wg[t] = keep.tile([P, S], F32, name=f"wg{t}")
             staged = []
             for hj in range(2):
-                st = head.tile([P, 4, 4, 32], F32, name=f"staged{t}{hj}", align_bytes=64, offset=(12288, 12288, 8192, 12288)[t] + 2048 * hj)
+                place = (WGS_AT if t == 2 else STAGE_AT) + 4 * BANK * hj
+                stage = head.tile([P, 4, 4, 32], F32, name=f"staged{t}{hj}", align_bytes=64, offset=place)
                 picked = turned[hj][:].rearrange("p c (q t) -> p c t q", t=PACK)[:, :, t : t + 1, :]
-                nc.scalar.copy(out=st[:], in_=picked.to_broadcast([P, 4, 4, 32]))
-                staged.append(st)
+                nc.scalar.copy(out=stage[:], in_=picked.to_broadcast([P, 4, 4, 32]))
+                staged.append(stage)
             for hj in range(2):
-                back = psum.tile([P, 4, P], F32, name=f"back{t}{hj}", tag=f"bank{(0, 2, 6, 6)[t] + hj}")
+                back = psum.tile([P, 4, P], F32, name=f"back{t}{hj}", tag=f"bank{(2 * t if t < 2 else 6) + hj}")
                 for c in range(4):
                     nc.tensor.transpose(back[:, c, :], staged[hj][:, c, :, :].rearrange("p d q -> p (d q)"), ident[:])
                 nc.scalar.copy(out=wg[t][:, BANK * hj : BANK * (hj + 1)], in_=back[:].rearrange("p c j -> p (c j)"))
 
-        def floor_h(i, halves=(0, 1)):
+        def floor_half(i, hj, dst):
             b, t = divmod(i, PACK)
-            if i not in hs:
-                hs[i] = hreg.tile([P, S], F32, name=f"h{i}", align_bytes=64, offset=H_AT[i])
-            for hj in halves:
-                cols = slice(BANK * hj, BANK * (hj + 1))
-                acc = psum.tile([P, BANK], F32, name=f"hacc{i}_{hj}", tag=f"bank{2 * (i % 4) + hj}")
-                for a in range(2):
-                    codes, scales = w1q[a, b]
-                    nc.tensor.matmul_mx(out=acc[:], lhsT=codes[:, P * t : P * (t + 1)].bitcast(FP8X4), lhsT_scale=scales[:, P * t : P * (t + 1)],
-                                        rhs=gw[a, hj].bitcast(FP8X4), rhs_scale=gs[4 * a : P, cols], start=(a == 0), stop=(a == 1))
-                nc.vector.tensor_tensor(out=hs[i][:, cols], in0=acc[:], in1=lows[i][:, cols], op=ALU.max)
+            cols = slice(BANK * hj, BANK * (hj + 1))
+            acc = psum.tile([P, BANK], F32, name=f"hacc{i}_{hj}", tag=f"bank{2 * (i % 4) + hj}")
+            for a in range(2):
+                codes, scales = w1q[a, b]
+                nc.tensor.matmul_mx(out=acc[:], lhsT=codes[:, P * t : P * (t + 1)].bitcast(FP8X4), lhsT_scale=scales[:, P * t : P * (t + 1)],
+                                    rhs=words[a, hj].bitcast(FP8X4), rhs_scale=picked_scales[4 * a : P, cols], start=(a == 0), stop=(a == 1))
+            nc.vector.tensor_tensor(out=dst, in0=acc[:], in1=lows[i][:, cols], op=ALU.max)
 
-        def scatter(i, first=0, last=S):
-            nc.vector.tensor_tensor(out=pages[i][:].indirect(o2[:, first // 16 : last // 16]), in0=hs[i][:, first:last],
-                                    in1=wg[i % PACK][:, first:last], op=ALU.mult)
+        def weigh_half(i, hj, dst):
+            nc.gpsimd.tensor_tensor(out=dst, in0=dst, in1=wg[i % PACK][:, BANK * hj : BANK * (hj + 1)], op=ALU.mult)
 
-        xi = {}
-        for which in (1, 2):
-            xi[which, 0] = [keep.tile([P, M, PACK], BF16, name=f"xi{which}0", align_bytes=64)]
-            xi[which, 1] = [keep.tile([P, HALF, PACK], BF16, name=f"xi{which}1{hm}", align_bytes=64) for hm in range(2)]
+        def weighted_h(i):
+            hs[i] = hreg.tile([P, S], F32, name=f"h{i}", align_bytes=64, offset=H_AT[i])
+            for hj in range(2):
+                dst = hs[i][:, BANK * hj : BANK * (hj + 1)]
+                floor_half(i, hj, dst)
+                weigh_half(i, hj, dst)
 
-        def plane(which, i, src):
+        def scatter(i):
+            nc.vector.tensor_copy(out=pages[i][:].indirect(list2[:]), in_=hs[i][:])
+
+        def put_place(which, i, src):
             b, t = divmod(i, PACK)
-            parts = xi[which, b]
-            w = M // len(parts)
+            parts = x_grouped[which, b]
+            width = M // len(parts)
             for n, part in enumerate(parts):
-                nc.scalar.activation(out=part[:, :, t], in_=src[:, w * n : w * (n + 1)], func=ACT.Copy, scale=col(f"gain{which}", i))
+                nc.scalar.activation(out=part[:, :, t], in_=src[:, width * n : width * (n + 1)], func=ACT.Copy, scale=col(f"gain{which}", i))
 
         def look(i):
             xs[i] = ring.tile([P, M], F32, name=f"x{i}", tag="x")
-            nc.scalar.activation(out=xs[i][:], in_=pages[i][:].indirect(o3[:]), func=ACT.Sigmoid, bias=col("cal_b", i), scale=col("cal_s", i))
-            plane(1, i, xs[i])
+            nc.scalar.activation(out=xs[i][:], in_=pages[i][:].indirect(list3[:]), func=ACT.Sigmoid, bias=col("cal_b", i), scale=col("cal_s", i))
+            put_place(1, i, xs[i])
 
-        def less_ease(i, engine):
-            if i < 6:
-                d = hreg.tile([P, M], F32, name=f"d{i}", align_bytes=64, offset=H_AT[i + 1] + D_AT)
-            else:
-                d = keep.tile([P, M], F32, name=f"d{i}")
-            engine.tensor_tensor(out=d[:], in0=xs[i][:], in1=eases[i][:], op=ALU.subtract)
-            plane(2, i, d)
-
-        deal_wgs(0)
-        for hj in range(2):
-            floor_h(0, (hj,))
-            scatter(0, BANK * hj, BANK * (hj + 1))
-        for t in range(1, PACK):
-            deal_wgs(t)
-
-        load_low(1)
-        load_low(2)
-        load_page(1)
-        floor_h(1)
-        floor_h(2)
-        scatter(1)
-
-        raw01 = load_raw(w1_part(0, 1), "raw1", "raw01")
-        raw11 = load_raw(w1_part(1, 1), "raw0", "raw11")
-        o3 = load_list(offs3, "o3")
-        load_vec("cal_s", cal_s)
-        load_vec("cal_b", cal_b)
-        load_low(3)
-        load_vec("gain1", gain1)
-        load_ease(0)
-        load_vec("gain2", gain2)
-        load_page(2)
-        g01 = group_w1(raw01, wbf("g01"), on_scalar)
-        g11 = group_w1(raw11, wbf("g11"), on_scalar)
-        look(0)
-        look(1)
-        floor_h(3)
-        less_ease(0, nc.gpsimd)
-        w1q[0, 1] = quantise(g01[:], "w1q01", H_AT[1] + PLANE_AT[0])
-        w1q[1, 1] = quantise(g11[:], "w1q11", H_AT[1] + PLANE_AT[1])
-        scatter(2)
-
-        load_low(4)
-        load_ease(1)
-        load_page(3)
-        look(2)
-        floor_h(4)
-        less_ease(1, nc.gpsimd)
-        scatter(3)
-
-        load_low(5)
-        load_ease(2)
-        load_page(4)
-        look(3)
-        floor_h(5)
-        less_ease(2, nc.gpsimd)
-        scatter(4)
-
-        load_low(6)
-        load_ease(3)
-        raw30 = load_raw(w3[0:KP, :], "tab0", "raw30")
-        w2w = keep.tile([P, 2, 2 * N], U8, name="w2w", align_bytes=64)
-        nc.sync.dma_start(out=w2w[:].bitcast(I32), in_=w2_words.rearrange("a p c -> p a c").bitcast(I32))
-        load_page(5)
-        for q in range(4):
-            nc.sync.dma_start(out=w2s[32 * q : 32 * q + 4, :, :].bitcast(I32),
-                              in_=w2_scales[:, 4 * q : 4 * q + 4, :].rearrange("a r c -> r a c").bitcast(I32))
-        look(4)
-        floor_h(6)
-        less_ease(3, nc.gpsimd)
-        g30 = group_w3(raw30, "g30")
-        scatter(5)
-
-        load_low(7)
-        load_ease(4)
-        raw31 = load_raw(w3[KP : 2 * KP, :], "tab1", "raw31")
-        load_page(6)
-        look(5)
-        floor_h(7)
-        less_ease(4, nc.gpsimd)
-        g31 = group_w3(raw31, "g31")
-        scatter(6)
-
-        load_ease(5)
-        load_ease(6)
-        load_page(7)
-        look(6)
-        less_ease(5, nc.vector)
-        xq = {}
-        for which in (1, 2):
-            codes, scales = quantise(xi[which, 0][0][:].rearrange("p m t -> p (m t)"), f"xq{which}0", H_AT[6] + PLANE_AT[which - 1])
-            for hm in range(2):
-                xq[which, 0, hm] = (codes[:, HALF * hm : HALF * (hm + 1)], scales[:, HALF * hm : HALF * (hm + 1)])
-        less_ease(6, nc.vector)
-        scatter(7)
-
-        load_ease(7)
-        w3q = [quantise(g30[:], "w3q0", H_AT[7] + PLANE_AT[0]), quantise(g31[:], "w3q1", H_AT[7] + PLANE_AT[1])]
-
-        yacc = {}
+        def less_ease(i):
+            nc.gpsimd.tensor_tensor(out=eases[i][:], in0=xs[i][:], in1=eases[i][:], op=ALU.subtract)
+            put_place(2, i, eases[i])
 
         def y_pass(which, b, hm):
             codes, scales = xq[which, b, hm]
@@ -316,36 +180,149 @@ def tile_list_tablature_fingering_kernel(tc, tab_words, tab_scales, offs, w1, lo
                 for u in range(2):
                     nt = 2 * pair + u
                     if which == 1:
-                        w = w2w[:, b, 2 * P * nt : 2 * P * (nt + 1)].bitcast(FP4X4)
-                        ws = w2s[:, b, P * nt : P * (nt + 1)]
+                        w_codes = w2w[:, b, 2 * P * nt : 2 * P * (nt + 1)].bitcast(FP4X4)
+                        w_scales = w2s[:, b, P * nt : P * (nt + 1)]
                     else:
-                        w = w3q[b][0][:, P * nt : P * (nt + 1)].bitcast(FP8X4)
-                        ws = w3q[b][1][:, P * nt : P * (nt + 1)]
-                    nc.tensor.matmul_mx(out=yacc[which, hm, pair][:, u, :], lhsT=w, lhsT_scale=ws, rhs=codes.bitcast(FP8X4), rhs_scale=scales,
+                        w_codes = w3q[b][0][:, P * nt : P * (nt + 1)].bitcast(FP8X4)
+                        w_scales = w3q[b][1][:, P * nt : P * (nt + 1)]
+                    nc.tensor.matmul_mx(out=yacc[which, hm, pair][:, u, :], lhsT=w_codes, lhsT_scale=w_scales, rhs=codes.bitcast(FP8X4), rhs_scale=scales,
                                         start=(b == 0 and u == 0), stop=(b == 1 and u == 1))
 
+        ident = keep.tile([P, P], F32, name="ident")
+        make_identity(nc, ident[:])
+        tab_s = head.tile([P, T], U8, name="tab_s", align_bytes=64, offset=TAB_SCALES_AT)
+        nc.vector.memset(tab_s[:].bitcast(U32), 0)
+        for q in range(4):
+            nc.scalar.dma_start(out=tab_s[32 * q : 32 * q + 8, :].bitcast(I32), in_=tab_scales[:, 4 * q : 4 * q + 4, :].bitcast(I32))
+        w2s = keep.tile([P, 2, N], U8, name="w2s", align_bytes=64)
+        nc.vector.memset(w2s[:].rearrange("p a c -> p (a c)").bitcast(U32), 0)
+
+        list1 = load_list(offs, "list1")
+        tab0 = load_tab(0)
+        wgs_rows = head.tile([P, S], F32, name="wgs_rows", align_bytes=64, offset=WGS_AT)
+        nc.sync.dma_start(out=wgs_rows[:], in_=wgs)
+        raw00 = load_raw(w1_part(0, 0), "raw0", "raw00")
+        raw10 = load_raw(w1_part(1, 0), "raw1", "raw10")
+        tab1 = load_tab(1)
+        list2 = load_list(offs2, "list2")
+        load_low(0, slice(0, BANK))
+        load_page(0)
+        load_low(0, slice(BANK, S))
+
+        gather_words(tab0, 0, keep.tile([P, S], U32, name="words0", align_bytes=64))
+        picked_scales = keep.tile([P, S], U8, name="picked_scales", align_bytes=64)
+        nc.vector.tensor_copy(out=picked_scales[:], in_=tab_s[:].indirect(list1[:]))
+        g00 = group_w1(raw00, grouped_tile("g00"), nc.scalar.copy)
+        g10 = group_w1(raw10, head.tile([P, PACK * KP], BF16, name="g10", align_bytes=64, offset=W1_GROUPED_AT), nc.vector.tensor_copy)
+        w1q[0, 0] = quantise(g00[:], "w1q00")
+        w1q[1, 0] = quantise(g10[:], "w1q10")
+        gather_words(tab1, 1, head.tile([P, S], U32, name="words1", align_bytes=64, offset=WORDS1_AT))
+
+        turned = []
+        for hj in range(2):
+            bank = psum.tile([P, 4, P], F32, name=f"turned{hj}", tag=f"bank{4 + hj}")
+            for c in range(4):
+                nc.tensor.transpose(bank[:, c, :], wgs_rows[:, BANK * hj + P * c : BANK * hj + P * (c + 1)], ident[:])
+            turned.append(bank)
+
+        x_grouped = {}
+        for which in (1, 2):
+            x_grouped[which, 0] = [keep.tile([P, M, PACK], BF16, name=f"xi{which}0", align_bytes=64)]
+            x_grouped[which, 1] = [keep.tile([P, HALF, PACK], BF16, name=f"xi{which}1{hm}", align_bytes=64) for hm in range(2)]
+
+        deal_wgs(0)
+        h0 = [hreg.tile([P, BANK], F32, name=f"h0{hj}", align_bytes=64, offset=H_AT[0] + 4 * BANK * hj) for hj in range(2)]
+        floor_half(0, 0, h0[0][:])
+        nc.vector.tensor_tensor(out=pages[0][:].indirect(list2[:, 0:LIST_HALF]), in0=h0[0][:], in1=wg[0][:, 0:BANK], op=ALU.mult)
+        floor_half(0, 1, h0[1][:])
+        weigh_half(0, 1, h0[1][:])
+        for t in range(1, PACK):
+            deal_wgs(t)
+        load_low(1)
+        weighted_h(1)
+        nc.vector.tensor_copy(out=pages[0][:].indirect(list2[:, LIST_HALF : 2 * LIST_HALF]), in_=h0[1][:])
+
+        load_low(2)
+        load_page(1)
+        weighted_h(2)
+        scatter(1)
+
+        raw01 = load_raw(w1_part(0, 1), "raw1", "raw01")
+        raw11 = load_raw(w1_part(1, 1), "raw0", "raw11")
+        list3 = load_list(offs3, "list3")
+        load_vec("cal_s", cal_s)
+        load_vec("cal_b", cal_b)
+        load_low(3)
+        load_vec("gain1", gain1)
+        load_ease(0)
+        load_vec("gain2", gain2)
+        load_page(2)
+        load_ease(1)
+        g01 = group_w1(raw01, grouped_tile("g01"), nc.scalar.copy)
+        g11 = group_w1(raw11, grouped_tile("g11"), nc.scalar.copy)
+        for i in range(2):
+            look(i)
+            less_ease(i)
+        w1q[0, 1] = quantise(g01[:], "w1q01", H_AT[1] + PLANE_AT[0])
+        w1q[1, 1] = quantise(g11[:], "w1q11", H_AT[1] + PLANE_AT[1])
+        weighted_h(3)
+        scatter(2)
+
+        w3_grouped = []
+        for i in range(3, TILES):
+            w3_pass = i - W3_STEP
+            if i + 1 < TILES:
+                load_low(i + 1)
+            if w3_pass in (0, 1):
+                w3_raw = load_raw(w3[KP * w3_pass : KP * (w3_pass + 1), :], f"tab{w3_pass}", f"raw3{w3_pass}")
+            if i == W3_STEP:
+                w2w = keep.tile([P, 2, 2 * N], U8, name="w2w", align_bytes=64)
+                nc.sync.dma_start(out=w2w[:].bitcast(I32), in_=w2_words.rearrange("a p c -> p a c").bitcast(I32))
+            load_ease(i - 1)
+            load_page(i)
+            if i == W3_STEP:
+                for q in range(4):
+                    nc.sync.dma_start(out=w2s[32 * q : 32 * q + 4, :, :].bitcast(I32),
+                                      in_=w2_scales[:, 4 * q : 4 * q + 4, :].rearrange("a r c -> r a c").bitcast(I32))
+            look(i - 1)
+            less_ease(i - 1)
+            if i + 1 < TILES:
+                weighted_h(i + 1)
+            else:
+                for which in (1, 2):
+                    codes, scales = quantise(x_grouped[which, 0][0][:].rearrange("p m t -> p (m t)"), f"xq{which}0", H_AT[i - 1] + PLANE_AT[which - 1])
+                    for hm in range(2):
+                        xq[which, 0, hm] = (codes[:, HALF * hm : HALF * (hm + 1)], scales[:, HALF * hm : HALF * (hm + 1)])
+            if w3_pass in (0, 1):
+                w3_grouped.append(group_w3(w3_raw, f"g3{w3_pass}"))
+            scatter(i)
+
+        last = TILES - 1
+        load_ease(last)
+        w3q = [quantise(w3_grouped[b][:], f"w3q{b}", H_AT[last] + PLANE_AT[b]) for b in range(2)]
         for which in (1, 2):
             for hm in range(2):
                 y_pass(which, 0, hm)
 
-        look(7)
-        d7 = [keep.tile([P, HALF], F32, name=f"d7{hm}") for hm in range(2)]
+        look(last)
+        diff = [keep.tile([P, HALF], F32, name=f"diff{hm}") for hm in range(2)]
         for hm in range(2):
             cols = slice(HALF * hm, HALF * (hm + 1))
-            nc.vector.tensor_tensor(out=d7[hm][:], in0=xs[7][:, cols], in1=eases[7][:, cols], op=ALU.subtract)
+            nc.vector.tensor_tensor(out=diff[hm][:], in0=xs[last][:, cols], in1=eases[last][:, cols], op=ALU.subtract)
         for hm in range(2):
-            nc.vector.tensor_scalar(out=xi[2, 1][hm][:, :, 3], in0=d7[hm][:], scalar1=col("gain2", 7), scalar2=None, op0=ALU.mult)
+            nc.vector.tensor_scalar(out=x_grouped[2, 1][hm][:, :, PACK - 1], in0=diff[hm][:], scalar1=col("gain2", last), scalar2=None, op0=ALU.mult)
         for hm in range(2):
             for which in (2, 1):
-                codes, scales = quantise(xi[which, 1][hm][:].rearrange("p m t -> p (m t)"), f"xq{which}1{hm}")
+                codes, scales = quantise(x_grouped[which, 1][hm][:].rearrange("p m t -> p (m t)"), f"xq{which}1{hm}")
                 xq[which, 1, hm] = (codes[:], scales[:])
                 y_pass(which, 1, hm)
+
         for hm in range(2):
             for pair in range(2):
                 res = keep.tile([P, 2, HALF], F32, name=f"res{hm}{pair}")
                 nc.scalar.copy(out=res[:], in_=yacc[2, hm, pair][:])
                 dst = out[2 * P * pair : 2 * P * (pair + 1), HALF * hm : HALF * (hm + 1)].rearrange("(u p) m -> p u m", u=2)
                 pieces = [slice(0, 1), slice(1, 2)] if (hm, pair) == (1, 1) else [slice(0, 2)]
-                for n, u in enumerate(pieces):
-                    nc.vector.tensor_tensor(out=res[:, u, :], in0=yacc[1, hm, pair][:, u, :], in1=res[:, u, :], op=ALU.mult)
-                    (nc.sync, nc.scalar)[n].dma_start(out=dst[:, u, :], in_=res[:, u, :])
+                for queue, us in zip((nc.sync, nc.scalar), pieces):
+                    nc.vector.tensor_tensor(out=res[:, us, :], in0=yacc[1, hm, pair][:, us, :], in1=res[:, us, :], op=ALU.mult)
+                    queue.dma_start(out=dst[:, us, :], in_=res[:, us, :])

from contextlib import ExitStack

import concourse.mybir as mybir
from concourse.masks import make_identity

K, T, S, H, T2, M, N = 1024, 2048, 1024, 1024, 2048, 512, 512
FLOPS = 2 * K * H * S + 2 * 2 * H * N * M

F32 = mybir.dt.float32
BF16 = mybir.dt.bfloat16
I32 = mybir.dt.int32
U32 = mybir.dt.uint32
U16 = mybir.dt.uint16
U8 = mybir.dt.uint8
FP8X4 = mybir.dt.float8_e4m3fn_x4
FP4X4 = mybir.dt.float4_e2m1fn_x4
ACT = mybir.ActivationFunctionType
ALU = mybir.AluOpType

P = 128
PACK = 4
KP = P * PACK
TILES = H // P
BANK = 512
LIST_HALF = BANK // 16
HALF = M // 2
W3_STEP = 5

H_STEP = 4 * S - 64
H_AT = [H_STEP * (4 + i // 2 if i % 2 == 0 else 3 - i // 2) for i in range(TILES)]
PLANE_AT = (2176, 2688)

W1_GROUPED_AT, TAB_SCALES_AT, WORDS1_AT, WGS_AT, STAGE_AT = 0, 3072, 4096, 8192, 12288


def tile_list_tablature_fingering_kernel(tc, tab_words, tab_scales, offs, w1, low, page0, wgs, offs2, offs3,
                                                   cal_s, cal_b, gain1, ease, gain2, w2_words, w2_scales, w3, out):
    nc = tc.nc
    with ExitStack() as ctx:
        keep = ctx.enter_context(tc.tile_pool(name="keep", bufs=1))
        ring = ctx.enter_context(tc.tile_pool(name="ring", bufs=4))
        bfp = ctx.enter_context(tc.tile_pool(name="bfp", bufs=2))
        hreg = ctx.enter_context(tc.tile_pool(name="hreg", bufs=1))
        head = ctx.enter_context(tc.tile_pool(name="head", bufs=1))
        psum = ctx.enter_context(tc.psum_pool(name="psum", bufs=1))

        lows, pages, eases, hs, xs, vec, words, wg, w1q, xq, yacc = {}, {}, {}, {}, {}, {}, {}, {}, {}, {}, {}

        def rows(mat, i):
            b, t = divmod(i, PACK)
            return mat.rearrange("(b p t) c -> b t p c", b=2, t=PACK)[b, t]

        def col(name, i):
            b, t = divmod(i, PACK)
            return vec[name][:, b, t : t + 1]

        def load_vec(name, src):
            vec[name] = keep.tile([P, 2, PACK], F32, name=name)
            nc.sync.dma_start(out=vec[name][:], in_=src.rearrange("(b p t) -> p b t", b=2, t=PACK))

        def load_list(src, name):
            tile = keep.tile([P, src.shape[1]], U16, name=name)
            nc.sync.dma_start(tile[:], src)
            return tile

        def load_tab(a):
            tile = keep.tile([P, T], I32, name=f"tabw{a}", tag=f"tab{a}")
            nc.sync.dma_start(out=tile[:], in_=tab_words[a].rearrange("p t i -> p (t i)").bitcast(I32))
            return tile

        def load_raw(src, tag, name):
            tile = keep.tile([P, PACK, KP], F32, name=name, tag=tag)
            nc.sync.dma_start(out=tile[:], in_=src.rearrange("(p j) c -> p j c", j=PACK))
            return tile

        def w1_part(a, b):
            return w1[KP * a : KP * (a + 1), KP * b : KP * (b + 1)]

        def load_low(i, cols=slice(0, S)):
            if i not in lows:
                lows[i] = ring.tile([P, S], F32, name=f"low{i}", tag="low")
            nc.sync.dma_start(out=lows[i][:, cols], in_=rows(low, i)[:, cols])

        def load_page(i):
            pages[i] = ring.tile([P, T2], F32, name=f"page{i}", tag="page")
            nc.sync.dma_start(out=pages[i][:], in_=rows(page0, i))

        def load_ease(i):
            eases[i] = keep.tile([P, M], F32, name=f"ease{i}")
            nc.sync.dma_start(out=eases[i][:], in_=rows(ease, i))

        def grouped_tile(name):
            return bfp.tile([P, PACK * KP], BF16, name=name, tag="wbf", align_bytes=64)

        def group_w1(raw, grouped, copy):
            copy(out=grouped[:].rearrange("p (t m j) -> p m j t", t=PACK, j=PACK),
                 in_=raw[:].rearrange("p j (m t) -> p m j t", t=PACK))
            return grouped

        def group_w3(raw, name):
            grouped = grouped_tile(name)
            nc.scalar.copy(out=grouped[:].rearrange("p (c n j) -> p c j n", n=4, j=PACK),
                           in_=raw[:].rearrange("p j (c n) -> p c j n", n=4))
            return grouped

        def quantise(grouped, name, plane_at=None):
            width = grouped.shape[1] // PACK
            codes = keep.tile([P, width], U32, name=name + "_codes", align_bytes=64)
            if plane_at is None:
                scales = keep.tile([P, width], U8, name=name + "_scales", align_bytes=64)
            else:
                scales = hreg.tile([P, width], U8, name=name + "_scales", align_bytes=64, offset=plane_at)
            nc.vector.quantize_mx(out=codes[:].bitcast(FP8X4), scales=scales[:], in_=grouped)
            return codes, scales

        def gather_words(tab, a, picked):
            for hj in range(2):
                words[a, hj] = picked[:, BANK * hj : BANK * (hj + 1)]
                nc.vector.tensor_copy(out=words[a, hj], in_=tab[:].bitcast(U32).indirect(list1[:, LIST_HALF * hj : LIST_HALF * (hj + 1)]))

        def deal_wgs(t):
            wg[t] = keep.tile([P, S], F32, name=f"wg{t}")
            staged = []
            for hj in range(2):
                place = (WGS_AT if t == 2 else STAGE_AT) + 4 * BANK * hj
                stage = head.tile([P, 4, 4, 32], F32, name=f"staged{t}{hj}", align_bytes=64, offset=place)
                picked = turned[hj][:].rearrange("p c (q t) -> p c t q", t=PACK)[:, :, t : t + 1, :]
                nc.scalar.copy(out=stage[:], in_=picked.to_broadcast([P, 4, 4, 32]))
                staged.append(stage)
            for hj in range(2):
                back = psum.tile([P, 4, P], F32, name=f"back{t}{hj}", tag=f"bank{(2 * t if t < 2 else 6) + hj}")
                for c in range(4):
                    nc.tensor.transpose(back[:, c, :], staged[hj][:, c, :, :].rearrange("p d q -> p (d q)"), ident[:])
                nc.scalar.copy(out=wg[t][:, BANK * hj : BANK * (hj + 1)], in_=back[:].rearrange("p c j -> p (c j)"))

        def floor_half(i, hj, dst):
            b, t = divmod(i, PACK)
            cols = slice(BANK * hj, BANK * (hj + 1))
            acc = psum.tile([P, BANK], F32, name=f"hacc{i}_{hj}", tag=f"bank{2 * (i % 4) + hj}")
            for a in range(2):
                codes, scales = w1q[a, b]
                nc.tensor.matmul_mx(out=acc[:], lhsT=codes[:, P * t : P * (t + 1)].bitcast(FP8X4), lhsT_scale=scales[:, P * t : P * (t + 1)],
                                    rhs=words[a, hj].bitcast(FP8X4), rhs_scale=picked_scales[4 * a : P, cols], start=(a == 0), stop=(a == 1))
            nc.vector.tensor_tensor(out=dst, in0=acc[:], in1=lows[i][:, cols], op=ALU.max)

        def weigh_half(i, hj, dst):
            nc.gpsimd.tensor_tensor(out=dst, in0=dst, in1=wg[i % PACK][:, BANK * hj : BANK * (hj + 1)], op=ALU.mult)

        def weighted_h(i):
            hs[i] = hreg.tile([P, S], F32, name=f"h{i}", align_bytes=64, offset=H_AT[i])
            for hj in range(2):
                dst = hs[i][:, BANK * hj : BANK * (hj + 1)]
                floor_half(i, hj, dst)
                weigh_half(i, hj, dst)

        def scatter(i):
            nc.vector.tensor_copy(out=pages[i][:].indirect(list2[:]), in_=hs[i][:])

        def put_place(which, i, src):
            b, t = divmod(i, PACK)
            parts = x_grouped[which, b]
            width = M // len(parts)
            for n, part in enumerate(parts):
                nc.scalar.activation(out=part[:, :, t], in_=src[:, width * n : width * (n + 1)], func=ACT.Copy, scale=col(f"gain{which}", i))

        def look(i):
            xs[i] = ring.tile([P, M], F32, name=f"x{i}", tag="x")
            nc.scalar.activation(out=xs[i][:], in_=pages[i][:].indirect(list3[:]), func=ACT.Sigmoid, bias=col("cal_b", i), scale=col("cal_s", i))
            put_place(1, i, xs[i])

        def less_ease(i):
            nc.gpsimd.tensor_tensor(out=eases[i][:], in0=xs[i][:], in1=eases[i][:], op=ALU.subtract)
            put_place(2, i, eases[i])

        def y_pass(which, b, hm):
            codes, scales = xq[which, b, hm]
            for pair in range(2):
                if b == 0:
                    yacc[which, hm, pair] = psum.tile([P, 2, HALF], F32, name=f"y{which}{hm}{pair}", tag=f"bank{4 * (which - 1) + 2 * hm + pair}")
                for u in range(2):
                    nt = 2 * pair + u
                    if which == 1:
                        w_codes = w2w[:, b, 2 * P * nt : 2 * P * (nt + 1)].bitcast(FP4X4)
                        w_scales = w2s[:, b, P * nt : P * (nt + 1)]
                    else:
                        w_codes = w3q[b][0][:, P * nt : P * (nt + 1)].bitcast(FP8X4)
                        w_scales = w3q[b][1][:, P * nt : P * (nt + 1)]
                    nc.tensor.matmul_mx(out=yacc[which, hm, pair][:, u, :], lhsT=w_codes, lhsT_scale=w_scales, rhs=codes.bitcast(FP8X4), rhs_scale=scales,
                                        start=(b == 0 and u == 0), stop=(b == 1 and u == 1))

        ident = keep.tile([P, P], F32, name="ident")
        make_identity(nc, ident[:])
        tab_s = head.tile([P, T], U8, name="tab_s", align_bytes=64, offset=TAB_SCALES_AT)
        nc.vector.memset(tab_s[:].bitcast(U32), 0)
        for q in range(4):
            nc.scalar.dma_start(out=tab_s[32 * q : 32 * q + 8, :].bitcast(I32), in_=tab_scales[:, 4 * q : 4 * q + 4, :].bitcast(I32))
        w2s = keep.tile([P, 2, N], U8, name="w2s", align_bytes=64)
        nc.vector.memset(w2s[:].rearrange("p a c -> p (a c)").bitcast(U32), 0)

        list1 = load_list(offs, "list1")
        tab0 = load_tab(0)
        wgs_rows = head.tile([P, S], F32, name="wgs_rows", align_bytes=64, offset=WGS_AT)
        nc.sync.dma_start(out=wgs_rows[:], in_=wgs)
        raw00 = load_raw(w1_part(0, 0), "raw0", "raw00")
        raw10 = load_raw(w1_part(1, 0), "raw1", "raw10")
        tab1 = load_tab(1)
        list2 = load_list(offs2, "list2")
        load_low(0, slice(0, BANK))
        load_page(0)
        load_low(0, slice(BANK, S))

        gather_words(tab0, 0, keep.tile([P, S], U32, name="words0", align_bytes=64))
        picked_scales = keep.tile([P, S], U8, name="picked_scales", align_bytes=64)
        nc.vector.tensor_copy(out=picked_scales[:], in_=tab_s[:].indirect(list1[:]))
        g00 = group_w1(raw00, grouped_tile("g00"), nc.scalar.copy)
        g10 = group_w1(raw10, head.tile([P, PACK * KP], BF16, name="g10", align_bytes=64, offset=W1_GROUPED_AT), nc.vector.tensor_copy)
        w1q[0, 0] = quantise(g00[:], "w1q00")
        w1q[1, 0] = quantise(g10[:], "w1q10")
        gather_words(tab1, 1, head.tile([P, S], U32, name="words1", align_bytes=64, offset=WORDS1_AT))

        turned = []
        for hj in range(2):
            bank = psum.tile([P, 4, P], F32, name=f"turned{hj}", tag=f"bank{4 + hj}")
            for c in range(4):
                nc.tensor.transpose(bank[:, c, :], wgs_rows[:, BANK * hj + P * c : BANK * hj + P * (c + 1)], ident[:])
            turned.append(bank)

        x_grouped = {}
        for which in (1, 2):
            x_grouped[which, 0] = [keep.tile([P, M, PACK], BF16, name=f"xi{which}0", align_bytes=64)]
            x_grouped[which, 1] = [keep.tile([P, HALF, PACK], BF16, name=f"xi{which}1{hm}", align_bytes=64) for hm in range(2)]

        deal_wgs(0)
        h0 = [hreg.tile([P, BANK], F32, name=f"h0{hj}", align_bytes=64, offset=H_AT[0] + 4 * BANK * hj) for hj in range(2)]
        floor_half(0, 0, h0[0][:])
        nc.vector.tensor_tensor(out=pages[0][:].indirect(list2[:, 0:LIST_HALF]), in0=h0[0][:], in1=wg[0][:, 0:BANK], op=ALU.mult)
        floor_half(0, 1, h0[1][:])
        weigh_half(0, 1, h0[1][:])
        for t in range(1, PACK):
            deal_wgs(t)
        load_low(1)
        weighted_h(1)
        nc.vector.tensor_copy(out=pages[0][:].indirect(list2[:, LIST_HALF : 2 * LIST_HALF]), in_=h0[1][:])

        load_low(2)
        load_page(1)
        weighted_h(2)
        scatter(1)

        raw01 = load_raw(w1_part(0, 1), "raw1", "raw01")
        raw11 = load_raw(w1_part(1, 1), "raw0", "raw11")
        list3 = load_list(offs3, "list3")
        load_vec("cal_s", cal_s)
        load_vec("cal_b", cal_b)
        load_low(3)
        load_vec("gain1", gain1)
        load_ease(0)
        load_vec("gain2", gain2)
        load_page(2)
        load_ease(1)
        g01 = group_w1(raw01, grouped_tile("g01"), nc.scalar.copy)
        g11 = group_w1(raw11, grouped_tile("g11"), nc.scalar.copy)
        for i in range(2):
            look(i)
            less_ease(i)
        w1q[0, 1] = quantise(g01[:], "w1q01", H_AT[1] + PLANE_AT[0])
        w1q[1, 1] = quantise(g11[:], "w1q11", H_AT[1] + PLANE_AT[1])
        weighted_h(3)
        scatter(2)

        w3_grouped = []
        for i in range(3, TILES):
            w3_pass = i - W3_STEP
            if i + 1 < TILES:
                load_low(i + 1)
            if w3_pass in (0, 1):
                w3_raw = load_raw(w3[KP * w3_pass : KP * (w3_pass + 1), :], f"tab{w3_pass}", f"raw3{w3_pass}")
            if i == W3_STEP:
                w2w = keep.tile([P, 2, 2 * N], U8, name="w2w", align_bytes=64)
                nc.sync.dma_start(out=w2w[:].bitcast(I32), in_=w2_words.rearrange("a p c -> p a c").bitcast(I32))
            load_ease(i - 1)
            load_page(i)
            if i == W3_STEP:
                for q in range(4):
                    nc.sync.dma_start(out=w2s[32 * q : 32 * q + 4, :, :].bitcast(I32),
                                      in_=w2_scales[:, 4 * q : 4 * q + 4, :].rearrange("a r c -> r a c").bitcast(I32))
            look(i - 1)
            less_ease(i - 1)
            if i + 1 < TILES:
                weighted_h(i + 1)
            else:
                for which in (1, 2):
                    codes, scales = quantise(x_grouped[which, 0][0][:].rearrange("p m t -> p (m t)"), f"xq{which}0", H_AT[i - 1] + PLANE_AT[which - 1])
                    for hm in range(2):
                        xq[which, 0, hm] = (codes[:, HALF * hm : HALF * (hm + 1)], scales[:, HALF * hm : HALF * (hm + 1)])
            if w3_pass in (0, 1):
                w3_grouped.append(group_w3(w3_raw, f"g3{w3_pass}"))
            scatter(i)

        last = TILES - 1
        load_ease(last)
        w3q = [quantise(w3_grouped[b][:], f"w3q{b}", H_AT[last] + PLANE_AT[b]) for b in range(2)]
        for which in (1, 2):
            for hm in range(2):
                y_pass(which, 0, hm)

        look(last)
        diff = [keep.tile([P, HALF], F32, name=f"diff{hm}") for hm in range(2)]
        for hm in range(2):
            cols = slice(HALF * hm, HALF * (hm + 1))
            nc.vector.tensor_tensor(out=diff[hm][:], in0=xs[last][:, cols], in1=eases[last][:, cols], op=ALU.subtract)
        for hm in range(2):
            nc.vector.tensor_scalar(out=x_grouped[2, 1][hm][:, :, PACK - 1], in0=diff[hm][:], scalar1=col("gain2", last), scalar2=None, op0=ALU.mult)
        for hm in range(2):
            for which in (2, 1):
                codes, scales = quantise(x_grouped[which, 1][hm][:].rearrange("p m t -> p (m t)"), f"xq{which}1{hm}")
                xq[which, 1, hm] = (codes[:], scales[:])
                y_pass(which, 1, hm)

        for hm in range(2):
            for pair in range(2):
                res = keep.tile([P, 2, HALF], F32, name=f"res{hm}{pair}")
                nc.scalar.copy(out=res[:], in_=yacc[2, hm, pair][:])
                dst = out[2 * P * pair : 2 * P * (pair + 1), HALF * hm : HALF * (hm + 1)].rearrange("(u p) m -> p u m", u=2)
                pieces = [slice(0, 1), slice(1, 2)] if (hm, pair) == (1, 1) else [slice(0, 2)]
                for queue, us in zip((nc.sync, nc.scalar), pieces):
                    nc.vector.tensor_tensor(out=res[:, us, :], in0=yacc[1, hm, pair][:, us, :], in1=res[:, us, :], op=ALU.mult)
                    queue.dma_start(out=dst[:, us, :], in_=res[:, us, :])
